import numpy as np
import ml_dtypes


def mxq(x, axis, fmt="e4m3"):
    dtype, down = {"e4m3": (ml_dtypes.float8_e4m3fn, 7), "e5m2": (ml_dtypes.float8_e5m2, 14)}[fmt]
    v = np.moveaxis(np.asarray(x, np.float32).astype(ml_dtypes.bfloat16).astype(np.float64), axis, -1)
    blocks = v.reshape(v.shape[:-1] + (-1, 32))
    amax = np.abs(blocks).max(-1, keepdims=True)
    byte = np.maximum(np.where(amax > 0, np.frexp(amax)[1] - 1 + 127, 0) - down, 1)
    scale = np.exp2(byte - 127.0)
    codes = (blocks / scale).astype(np.float32).astype(dtype).astype(np.float64)
    return np.moveaxis((codes * scale).reshape(v.shape), -1, axis)


WIDE = False


def mx_kscale(k):
    if not WIDE:
        return np.ones(k)
    levels = np.array([24, -24, 12, -12, 0])
    if k % 512:
        return np.exp2(np.random.permutation(np.resize(levels, k // 32))).repeat(32)
    a = np.empty((k // 512, 16))
    for p in range(k // 512):
        a[p, :8] = np.random.permutation(np.resize(levels, 8))
        for g in range(8):
            far = levels[np.abs(levels - a[p, g]) >= 10]
            a[p, g + 8] = far[np.random.randint(len(far))]
    return np.exp2(a.ravel()).repeat(32)


def f64(x):
    return np.asarray(x).astype(np.float64)


def striped(idx):
    return np.tile(idx.reshape(-1, 16).T, (8, 1)).astype(np.uint16)


def unstriped(offs):
    return offs[:16].T.reshape(-1).astype(np.int64)


E2M1 = np.array([0.0, 0.5, 1.0, 1.5, 2.0, 3.0, 4.0, 6.0, -0.0, -0.5, -1.0, -1.5, -2.0, -3.0, -4.0, -6.0])


def pack_weight(w, fmt):
    k, n = w.shape
    w = f64(np.asarray(w, np.float32).astype(ml_dtypes.bfloat16)).reshape(k // 32, 32, n)
    amax = np.abs(w).max(1)
    if fmt == "e4m3":
        byte = np.frexp(amax)[1] - 1 + 127 - 7
    else:
        mant, ex = np.frexp(amax / 6.0)
        byte = np.where(mant > 0.5, ex, ex - 1) + 127
    byte = np.clip(np.where(amax > 0, byte, 1), 1, 254)
    scaled = (w * np.exp2(127.0 - byte)[:, None, :]).reshape(k, n).astype(np.float32)
    by_word = np.ascontiguousarray(scaled.reshape(k // 512, 128, 4, n).transpose(0, 1, 3, 2))
    if fmt == "e4m3":
        words = by_word.astype(ml_dtypes.float8_e4m3fn).view(np.uint8)
    else:
        c = by_word.astype(ml_dtypes.float4_e2m1fn).view(np.uint8) & 0xF
        words = (c[..., 0::2] | (c[..., 1::2] << 4)).reshape(k // 512, 128, 2 * n)
    return np.ascontiguousarray(words), np.ascontiguousarray(byte.astype(np.uint8).reshape(k // 512, 16, n))


def unpack_weight(words, scales, fmt):
    g, _, n = scales.shape
    words = np.ascontiguousarray(words).reshape(g, 128, n, -1)
    if fmt == "e4m3":
        vals = words.view(ml_dtypes.float8_e4m3fn).astype(np.float64)
    else:
        nib = np.empty((g, 128, n, 4), np.uint8)
        nib[..., 0::2] = words & 0xF
        nib[..., 1::2] = words >> 4
        vals = E2M1[nib]
    vals = vals * np.repeat(np.exp2(scales.astype(np.float64) - 127.0), 8, axis=1)[..., None]
    return vals.transpose(0, 1, 3, 2).reshape(g * 512, n)


def pack_table4(v):
    words, scales = pack_weight(v, "e2m1")
    g, t = words.shape[0] // 2, v.shape[1]
    return np.ascontiguousarray(words.reshape(g, 2, 128, t, 2).transpose(0, 2, 3, 1, 4).reshape(g, 128, t, 4)), scales


def unpack_table4(words, scales):
    g, _, t, _ = words.shape
    return unpack_weight(words.reshape(g, 128, t, 2, 2).transpose(0, 3, 1, 2, 4).reshape(2 * g, 128, 2 * t), scales, "e2m1")


K, R, T, M, J = 1024, 1024, 2048, 1024, 1024


def setup_inputs():
    n = np.random.standard_normal
    s = mx_kscale(K)[:, None]
    u = mx_kscale(R)[:, None]
    p_tab = pack_weight(n((K, T)) * s, "e4m3")
    p_tab2 = pack_table4(n((K, T)) * s)
    p_wa = pack_weight(n((K, R)) / np.sqrt(K) / s * u.T, "e4m3")
    p_wb = pack_weight(n((K, R)) / np.sqrt(K) / s / u.T, "e4m3")
    return {
        "tab_words": p_tab[0],
        "tab_scales": p_tab[1],
        "tab2_words": p_tab2[0],
        "tab2_scales": p_tab2[1],
        "wa_words": p_wa[0],
        "wa_scales": p_wa[1],
        "wb_words": p_wb[0],
        "wb_scales": p_wb[1],
        "pr": (n((M, J))).astype(np.float32),
        "offs": striped(np.random.permutation(T)[:M]),
        "offs2": striped(np.random.permutation(T)[:J]),
    }


def reference(tab_words, tab_scales, tab2_words, tab2_scales, wa_words, wa_scales, wb_words, wb_scales, pr, offs, offs2):
    idx = unstriped(offs)
    idx2 = unstriped(offs2)
    tab_ = unpack_weight(tab_words, tab_scales, "e4m3")[:, idx]
    tab2_ = unpack_table4(tab2_words, tab2_scales)[:, idx2]
    wa_ = unpack_weight(wa_words, wa_scales, "e4m3")
    wb_ = unpack_weight(wb_words, wb_scales, "e4m3")
    za = wa_.T @ tab_
    zb = wb_.T @ tab2_
    ha = za
    hb = zb
    ha_ = mxq(ha, 0, "e4m3")
    hb_ = mxq(hb, 0, "e4m3")
    y = ha_.T @ hb_
    return y * 0.03125 + f64(pr)

@@ -1,0 +1,250 @@
+from contextlib import ExitStack
+
+import concourse.mybir as mybir
+
+K, R, T, M, J = 1024, 1024, 2048, 1024, 1024
+FLOPS = 2 * K * R * M + 2 * K * R * J + 2 * R * M * J
+
+F32 = mybir.dt.float32
+BF16 = mybir.dt.bfloat16
+I32 = mybir.dt.int32
+U32 = mybir.dt.uint32
+U16 = mybir.dt.uint16
+U8 = mybir.dt.uint8
+FP8X4 = mybir.dt.float8_e4m3fn_x4
+FP4X4 = mybir.dt.float4_e2m1fn_x4
+MULT = mybir.AluOpType.mult
+ADD = mybir.AluOpType.add
+
+P = 128
+PACK = 4
+PASSES = 2
+GROUPS = 2
+RUN = 8
+BLOCKS = 16
+CH = 128
+LOOK = 256
+HALF = 512
+SCORE_SCALE = 0.03125
+LAG = 2
+
+
+def tile_list_biaff_none_prior_kernel(
+    tc, tab_words, tab_scales, tab2_words, tab2_scales, wa_words, wa_scales, wb_words, wb_scales, pr, offs, offs2, out
+):
+    nc = tc.nc
+    with ExitStack() as ctx:
+        keep = ctx.enter_context(tc.tile_pool(name="keep", bufs=1))
+        stage = ctx.enter_context(tc.tile_pool(name="stage", bufs=4))
+        psum1 = ctx.enter_context(tc.psum_pool(name="psum1", bufs=4))
+        psum2 = ctx.enter_context(tc.psum_pool(name="psum2", bufs=4))
+
+        def held(name, shape, dtype):
+            return keep.tile(shape, dtype, name=name, align_bytes=256)
+
+        list_a = keep.tile([P, M // 16], U16, name="list_a")
+        list_b = keep.tile([P, J // 16], U16, name="list_b")
+        ta_w = [held("ta_w%d" % a, [P, T], I32) for a in range(PASSES)]
+        ta_s = held("ta_s", [P, T // 4], I32)
+        tb_w = held("tb_w", [P, T], I32)
+        tb_s = held("tb_s", [P, T // 4], I32)
+        gb_rows = held("gb_rows", [P, J], U8)
+        wa_raw = [held("wa_raw%d" % g, [P, PASSES, HALF], I32) for g in range(GROUPS)]
+        wb_raw = [held("wb_raw%d" % g, [P, PASSES, HALF], I32) for g in range(GROUPS)]
+        wa_sraw = held("wa_sraw", [P, R // 4], I32)
+        wb_sraw = held("wb_sraw", [P, PASSES, R // 4], I32)
+        wa_w = [held("wa_w%d" % g, [P, PACK, PASSES, P], I32) for g in range(GROUPS)]
+        wb_w = [held("wb_w%d" % g, [P, PACK, PASSES, P], I32) for g in range(GROUPS)]
+        wa_s = held("wa_s", [P, PACK, GROUPS, P // 4], I32)
+        wb_s = held("wb_s", [P, PACK, PASSES, GROUPS, P // 4], I32)
+        ga_w = held("ga_w", [P, PASSES, M], U32)
+        ga_s = held("ga_s", [P, M], U8)
+        gb_pair = held("gb_pair", [P, J], U32)
+        gb_w = held("gb_w", [P, PASSES, 2 * J], U8)
+        gb_s = held("gb_s", [P, PASSES, J], U8)
+        hb16 = held("hb16", [P, GROUPS, J, PACK], BF16)
+        hb_w = held("hb_w", [P, GROUPS, J], U32)
+        hb_s = held("hb_s", [P, GROUPS, J], U8)
+        ha_w = held("ha_w", [P, M // CH, GROUPS, CH], U32)
+        ha_s = held("ha_s", [P, M // CH, GROUPS, CH], U8)
+        prior = [held("prior%d" % i, [P, J], F32) for i in range(M // CH)]
+
+        def words(src):
+            return src.rearrange("p n t -> p (n t)").bitcast(I32)
+
+        def load_weight(dst, src, g):
+            view = src.rearrange("a p n t -> p a (n t)").bitcast(I32)
+            nc.sync.dma_start(out=dst[:], in_=view[:, :, g * HALF : (g + 1) * HALF])
+
+        def load_scales_apart(queue, dst, src):
+            rows = src.bitcast(I32)
+            for q in range(4):
+                queue.dma_start(
+                    out=dst[32 * q : 32 * q + 4, :, :], in_=rows[:, 4 * q : 4 * q + 4, :].rearrange("a r n -> r a n")
+                )
+
+        def load_scales_packed(queue, dst, src):
+            rows = src.bitcast(I32)
+            for q in range(4):
+                queue.dma_start(out=dst[32 * q : 32 * q + 8, :], in_=rows[:, 4 * q : 4 * q + 4, :])
+
+        nc.vector.memset(wb_sraw[:], 0)
+        nc.vector.memset(tb_s[32:64, :], 0)
+        nc.vector.memset(tb_s[64:128, :], 0)
+        nc.vector.memset(gb_s[:].bitcast(I32), 0)
+        nc.vector.memset(ta_s[:], 0)
+        nc.vector.memset(wa_sraw[:], 0)
+
+        nc.sync.dma_start(list_b[:], offs2)
+        nc.sync.dma_start(out=tb_s[0:32, :], in_=tab2_scales.bitcast(I32).rearrange("a q n -> q a n"))
+        load_scales_apart(nc.scalar, wb_sraw, wb_scales)
+        load_weight(wb_raw[0], wb_words, 0)
+        nc.sync.dma_start(out=tb_w[:], in_=words(tab2_words[0]))
+        load_weight(wb_raw[1], wb_words, 1)
+        nc.sync.dma_start(list_a[:], offs)
+        for a in range(PASSES):
+            nc.sync.dma_start(out=ta_w[a][:], in_=words(tab_words[a]))
+        load_weight(wa_raw[0], wa_words, 0)
+        load_weight(wa_raw[1], wa_words, 1)
+        for i in range(M // CH):
+            nc.sync.dma_start(out=prior[i][:], in_=pr[i * CH : (i + 1) * CH, :])
+
+        def reorder_words(dst, raw):
+            nc.vector.tensor_copy(
+                out=dst[:].rearrange("p t a (b i) -> p t (a b) i", i=RUN),
+                in_=raw[:].rearrange("p a (b t i) -> p t (a b) i", t=PACK, i=RUN),
+            )
+
+        def reorder_scales(dst_flat, raw_flat):
+            nc.vector.tensor_copy(
+                out=dst_flat.rearrange("p (t b i) -> p t b i", t=PACK, i=RUN // 4),
+                in_=raw_flat.rearrange("p (b t i) -> p t b i", t=PACK, i=RUN // 4),
+            )
+
+        def entries(lst, q):
+            return lst[:, q * LOOK // 16 : (q + 1) * LOOK // 16]
+
+        def gather_b_scales(h):
+            cols = slice(h * HALF, (h + 1) * HALF)
+            nc.vector.tensor_copy(
+                gb_rows[:, cols], tb_s[:].bitcast(U8).indirect(list_b[:, h * HALF // 16 : (h + 1) * HALF // 16])
+            )
+            for q in range(4):
+                nc.scalar.dma_start(
+                    out=gb_s[32 * q : 32 * q + 4, :, cols].bitcast(I32), in_=gb_rows[8 * q : 8 * q + 8, cols].bitcast(I32)
+                )
+
+        def gather_b_words(q):
+            cols = slice(q * LOOK, (q + 1) * LOOK)
+            nc.vector.tensor_copy(gb_pair[:, cols], tb_w[:].bitcast(U32).indirect(entries(list_b, q)))
+            nc.vector.tensor_copy(
+                out=gb_w[:].bitcast(U16)[:, :, cols],
+                in_=gb_pair[:, cols].bitcast(U16).rearrange("p (n d) -> p d n", d=PASSES),
+            )
+
+        def gather_a(q):
+            cols = slice(q * LOOK, (q + 1) * LOOK)
+            nc.vector.tensor_copy(ga_s[:, cols], ta_s[:].bitcast(U8).indirect(entries(list_a, q)))
+            for a in range(PASSES):
+                nc.vector.tensor_copy(ga_w[:, a, cols], ta_w[a][:].bitcast(U32).indirect(entries(list_a, q)))
+
+        def layer_b(c, g):
+            bank = psum1.tile([P, PACK, CH], F32, name="layer_bank")
+            for t in range(PACK):
+                for a in range(PASSES):
+                    nc.tensor.matmul_mx(
+                        out=bank[:, t, :],
+                        lhsT=wb_w[g][:, t, a, :].bitcast(FP8X4),
+                        lhsT_scale=wb_s[:, t, a, g, :].bitcast(U8),
+                        rhs=gb_w[:, a, 2 * c * CH : 2 * (c + 1) * CH].bitcast(FP4X4),
+                        rhs_scale=gb_s[:, a, c * CH : (c + 1) * CH],
+                        start=(a == 0),
+                        stop=(a == PASSES - 1),
+                    )
+            nc.scalar.copy(out=hb16[:, g, c * CH : (c + 1) * CH, :], in_=bank[:].rearrange("p t n -> p n t"))
+
+        def quantize_b(h, g):
+            cols = slice(h * HALF, (h + 1) * HALF)
+            nc.vector.quantize_mx(
+                out=hb_w[:, g, cols].bitcast(FP8X4),
+                scales=hb_s[:, g, cols],
+                in_=hb16[:, g, cols, :].rearrange("p n t -> p (n t)"),
+            )
+
+        def layer_a(c):
+            ha16 = stage.tile([P, GROUPS, CH, PACK], BF16, name="ha16", align_bytes=256)
+            for g in range(GROUPS):
+                bank = psum1.tile([P, PACK, CH], F32, name="layer_bank")
+                for t in range(PACK):
+                    for a in range(PASSES):
+                        nc.tensor.matmul_mx(
+                            out=bank[:, t, :],
+                            lhsT=wa_w[g][:, t, a, :].bitcast(FP8X4),
+                            lhsT_scale=wa_s[4 * a :, t, g, :].bitcast(U8),
+                            rhs=ga_w[:, a, c * CH : (c + 1) * CH].bitcast(FP8X4),
+                            rhs_scale=ga_s[4 * a :, c * CH : (c + 1) * CH],
+                            start=(a == 0),
+                            stop=(a == PASSES - 1),
+                        )
+                nc.scalar.copy(out=ha16[:, g, :, :], in_=bank[:].rearrange("p t n -> p n t"))
+            return ha16
+
+        def quantize_a(c, ha16):
+            nc.vector.quantize_mx(
+                out=ha_w[:, c, :, :].rearrange("p g n -> p (g n)").bitcast(FP8X4),
+                scales=ha_s[:, c, :, :].rearrange("p g n -> p (g n)"),
+                in_=ha16[:].rearrange("p g n t -> p (g n t)"),
+            )
+
+        def scores(c):
+            for h in range(J // HALF):
+                cols = slice(h * HALF, (h + 1) * HALF)
+                bank = psum2.tile([P, HALF], F32, name="score_bank")
+                for g in range(GROUPS):
+                    nc.tensor.matmul_mx(
+                        out=bank[:],
+                        lhsT=ha_w[:, c, g, :].bitcast(FP8X4),
+                        lhsT_scale=ha_s[:, c, g, :],
+                        rhs=hb_w[:, g, cols].bitcast(FP8X4),
+                        rhs_scale=hb_s[:, g, cols],
+                        start=(g == 0),
+                        stop=(g == GROUPS - 1),
+                    )
+                nc.vector.scalar_tensor_tensor(
+                    out=prior[c][:, cols], in0=bank[:], scalar=SCORE_SCALE, in1=prior[c][:, cols], op0=MULT, op1=ADD
+                )
+                nc.sync.dma_start(out=out[c * CH : (c + 1) * CH, cols], in_=prior[c][:, cols])
+
+        gather_b_scales(0)
+        gather_b_scales(1)
+        load_scales_packed(nc.scalar, ta_s, tab_scales)
+        load_scales_packed(nc.scalar, wa_sraw, wa_scales)
+        reorder_words(wb_w[0], wb_raw[0])
+        reorder_scales(wb_s[:].rearrange("p t a g n -> p (t a g n)"), wb_sraw[:].rearrange("p a n -> p (a n)"))
+        gather_b_words(0)
+        reorder_words(wb_w[1], wb_raw[1])
+        for q in range(J // LOOK):
+            if q + 1 < J // LOOK:
+                gather_b_words(q + 1)
+            else:
+                reorder_scales(wa_s[:].rearrange("p t g n -> p (t g n)"), wa_sraw[:])
+                reorder_words(wa_w[0], wa_raw[0])
+                gather_a(0)
+                reorder_words(wa_w[1], wa_raw[1])
+            for g in range(GROUPS):
+                for c in range(2 * q, 2 * q + 2):
+                    layer_b(c, g)
+
+        for c in range(M // CH + LAG):
+            if c % 2 == 0 and c // 2 + 1 < M // LOOK:
+                gather_a(c // 2 + 1)
+            if c < M // CH:
+                ha16 = layer_a(c)
+            if c == 0:
+                for h in range(J // HALF):
+                    for g in range(GROUPS):
+                        quantize_b(h, g)
+            if c >= LAG:
+                scores(c - LAG)
+            if c < M // CH:
+                quantize_a(c, ha16)

@@ -27,6 +27,8 @@ LOOK = 256
 HALF = 512
 SCORE_SCALE = 0.03125
 LAG = 2
+ROWS = 32
+ZERO_RUN = 256
 
 
 def tile_list_biaff_none_prior_kernel(
@@ -48,23 +50,24 @@ def tile_list_biaff_none_prior_kernel(
         ta_s = held("ta_s", [P, T // 4], I32)
         tb_w = held("tb_w", [P, T], I32)
         tb_s = held("tb_s", [P, T // 4], I32)
-        gb_rows = held("gb_rows", [P, J], U8)
         wa_raw = [held("wa_raw%d" % g, [P, PASSES, HALF], I32) for g in range(GROUPS)]
         wb_raw = [held("wb_raw%d" % g, [P, PASSES, HALF], I32) for g in range(GROUPS)]
-        wa_sraw = held("wa_sraw", [P, R // 4], I32)
-        wb_sraw = held("wb_sraw", [P, PASSES, R // 4], I32)
+        wa_sraw = held("wa_sraw", [ROWS, R // 4], I32)
+        wb_sraw = held("wb_sraw", [ROWS, R // 4], I32)
+        ga_s = held("ga_s", [P, M], U8)
+        gb_s = held("gb_s", [P, HALF], U8)
+        a_rows = held("a_rows", [ROWS, (R + M) // 4], I32)
+        b_rows = held("b_rows", [ROWS, (R + HALF) // 4], I32)
+        a_planes = held("a_planes", [P, PASSES, (R + M) // 4], I32)
+        b_planes = held("b_planes", [P, PASSES, (R + HALF) // 4], I32)
+        b_late = held("b_late", [P, PASSES, HALF // 4], I32)
         wa_w = [held("wa_w%d" % g, [P, PACK, PASSES, P], I32) for g in range(GROUPS)]
         wb_w = [held("wb_w%d" % g, [P, PACK, PASSES, P], I32) for g in range(GROUPS)]
-        wa_s = held("wa_s", [P, PACK, GROUPS, P // 4], I32)
-        wb_s = held("wb_s", [P, PACK, PASSES, GROUPS, P // 4], I32)
-        ga_w = held("ga_w", [P, PASSES, M], U32)
-        ga_s = held("ga_s", [P, M], U8)
-        gb_pair = held("gb_pair", [P, J], U32)
+        ga_first = held("ga_first", [P, PASSES, LOOK], U32)
+        gb_pair = [held("gb_pair%d" % q, [P, LOOK], U32) for q in range(J // LOOK)]
         gb_w = held("gb_w", [P, PASSES, 2 * J], U8)
-        gb_s = held("gb_s", [P, PASSES, J], U8)
         hb16 = held("hb16", [P, GROUPS, J, PACK], BF16)
-        hb_w = held("hb_w", [P, GROUPS, J], U32)
-        hb_s = held("hb_s", [P, GROUPS, J], U8)
+        hb_w = [held("hb_w%d" % h, [P, GROUPS, HALF], U32) for h in range(J // HALF)]
         ha_w = held("ha_w", [P, M // CH, GROUPS, CH], U32)
         ha_s = held("ha_s", [P, M // CH, GROUPS, CH], U8)
         prior = [held("prior%d" % i, [P, J], F32) for i in range(M // CH)]
@@ -76,38 +79,12 @@ def tile_list_biaff_none_prior_kernel(
             view = src.rearrange("a p n t -> p a (n t)").bitcast(I32)
             nc.sync.dma_start(out=dst[:], in_=view[:, :, g * HALF : (g + 1) * HALF])
 
-        def load_scales_apart(queue, dst, src):
-            rows = src.bitcast(I32)
+        def load_rows(queue, dst, src):
+            queue.dma_start(out=dst, in_=src.bitcast(I32).rearrange("a q n -> q a n"))
+
+        def spread_rows(planes, rows):
             for q in range(4):
-                queue.dma_start(
-                    out=dst[32 * q : 32 * q + 4, :, :], in_=rows[:, 4 * q : 4 * q + 4, :].rearrange("a r n -> r a n")
-                )
-
-        def load_scales_packed(queue, dst, src):
-            rows = src.bitcast(I32)
-            for q in range(4):
-                queue.dma_start(out=dst[32 * q : 32 * q + 8, :], in_=rows[:, 4 * q : 4 * q + 4, :])
-
-        nc.vector.memset(wb_sraw[:], 0)
-        nc.vector.memset(tb_s[32:64, :], 0)
-        nc.vector.memset(tb_s[64:128, :], 0)
-        nc.vector.memset(gb_s[:].bitcast(I32), 0)
-        nc.vector.memset(ta_s[:], 0)
-        nc.vector.memset(wa_sraw[:], 0)
-
-        nc.sync.dma_start(list_b[:], offs2)
-        nc.sync.dma_start(out=tb_s[0:32, :], in_=tab2_scales.bitcast(I32).rearrange("a q n -> q a n"))
-        load_scales_apart(nc.scalar, wb_sraw, wb_scales)
-        load_weight(wb_raw[0], wb_words, 0)
-        nc.sync.dma_start(out=tb_w[:], in_=words(tab2_words[0]))
-        load_weight(wb_raw[1], wb_words, 1)
-        nc.sync.dma_start(list_a[:], offs)
-        for a in range(PASSES):
-            nc.sync.dma_start(out=ta_w[a][:], in_=words(tab_words[a]))
-        load_weight(wa_raw[0], wa_words, 0)
-        load_weight(wa_raw[1], wa_words, 1)
-        for i in range(M // CH):
-            nc.sync.dma_start(out=prior[i][:], in_=pr[i * CH : (i + 1) * CH, :])
+                nc.sync.dma_start(out=planes[32 * q : 32 * q + 4, :, :], in_=rows[8 * q : 8 * q + 8, :])
 
         def reorder_words(dst, raw):
             nc.vector.tensor_copy(
@@ -124,40 +101,46 @@ def tile_list_biaff_none_prior_kernel(
         def entries(lst, q):
             return lst[:, q * LOOK // 16 : (q + 1) * LOOK // 16]
 
-        def gather_b_scales(h):
-            cols = slice(h * HALF, (h + 1) * HALF)
+        def gather_b_scales(dst, h):
             nc.vector.tensor_copy(
-                gb_rows[:, cols], tb_s[:].bitcast(U8).indirect(list_b[:, h * HALF // 16 : (h + 1) * HALF // 16])
+                dst[:],
+                tb_s[:].bitcast(U8).indirect(list_b[:, h * HALF // 16 : (h + 1) * HALF // 16]),
             )
-            for q in range(4):
-                nc.scalar.dma_start(
-                    out=gb_s[32 * q : 32 * q + 4, :, cols].bitcast(I32), in_=gb_rows[8 * q : 8 * q + 8, cols].bitcast(I32)
-                )
 
         def gather_b_words(q):
             cols = slice(q * LOOK, (q + 1) * LOOK)
-            nc.vector.tensor_copy(gb_pair[:, cols], tb_w[:].bitcast(U32).indirect(entries(list_b, q)))
+            nc.vector.tensor_copy(gb_pair[q][:], tb_w[:].bitcast(U32).indirect(entries(list_b, q)))
             nc.vector.tensor_copy(
                 out=gb_w[:].bitcast(U16)[:, :, cols],
-                in_=gb_pair[:, cols].bitcast(U16).rearrange("p (n d) -> p d n", d=PASSES),
+                in_=gb_pair[q][:].bitcast(U16).rearrange("p (n d) -> p d n", d=PASSES),
             )
 
+        def ga_cols(a, first, count):
+            if first < LOOK:
+                return ga_first[:, a, first : first + count]
+            return ga_rest[:, a, first - LOOK : first - LOOK + count]
+
         def gather_a(q):
-            cols = slice(q * LOOK, (q + 1) * LOOK)
-            nc.vector.tensor_copy(ga_s[:, cols], ta_s[:].bitcast(U8).indirect(entries(list_a, q)))
             for a in range(PASSES):
-                nc.vector.tensor_copy(ga_w[:, a, cols], ta_w[a][:].bitcast(U32).indirect(entries(list_a, q)))
+                nc.vector.tensor_copy(ga_cols(a, q * LOOK, LOOK), ta_w[a][:].bitcast(U32).indirect(entries(list_a, q)))
+
+        def weight_scale(planes, a, t, g):
+            first = (t * GROUPS + g) * P // 4
+            return planes[:, a, first : first + P // 4].bitcast(U8)
 
         def layer_b(c, g):
             bank = psum1.tile([P, PACK, CH], F32, name="layer_bank")
+            early = c * CH < HALF
+            planes = b_planes if early else b_late
+            first = (R + c * CH) // 4 if early else (c * CH - HALF) // 4
             for t in range(PACK):
                 for a in range(PASSES):
                     nc.tensor.matmul_mx(
                         out=bank[:, t, :],
                         lhsT=wb_w[g][:, t, a, :].bitcast(FP8X4),
-                        lhsT_scale=wb_s[:, t, a, g, :].bitcast(U8),
+                        lhsT_scale=weight_scale(b_planes, a, t, g),
                         rhs=gb_w[:, a, 2 * c * CH : 2 * (c + 1) * CH].bitcast(FP4X4),
-                        rhs_scale=gb_s[:, a, c * CH : (c + 1) * CH],
+                        rhs_scale=planes[:, a, first : first + CH // 4].bitcast(U8),
                         start=(a == 0),
                         stop=(a == PASSES - 1),
                     )
@@ -166,7 +149,7 @@ def tile_list_biaff_none_prior_kernel(
         def quantize_b(h, g):
             cols = slice(h * HALF, (h + 1) * HALF)
             nc.vector.quantize_mx(
-                out=hb_w[:, g, cols].bitcast(FP8X4),
+                out=hb_w[h][:, g, :].bitcast(FP8X4),
                 scales=hb_s[:, g, cols],
                 in_=hb16[:, g, cols, :].rearrange("p n t -> p (n t)"),
             )
@@ -180,9 +163,9 @@ def tile_list_biaff_none_prior_kernel(
                         nc.tensor.matmul_mx(
                             out=bank[:, t, :],
                             lhsT=wa_w[g][:, t, a, :].bitcast(FP8X4),
-                            lhsT_scale=wa_s[4 * a :, t, g, :].bitcast(U8),
-                            rhs=ga_w[:, a, c * CH : (c + 1) * CH].bitcast(FP8X4),
-                            rhs_scale=ga_s[4 * a :, c * CH : (c + 1) * CH],
+                            lhsT_scale=weight_scale(a_planes, a, t, g),
+                            rhs=ga_cols(a, c * CH, CH).bitcast(FP8X4),
+                            rhs_scale=a_planes[:, a, (R + c * CH) // 4 : (R + (c + 1) * CH) // 4].bitcast(U8),
                             start=(a == 0),
                             stop=(a == PASSES - 1),
                         )
@@ -205,7 +188,7 @@ def tile_list_biaff_none_prior_kernel(
                         out=bank[:],
                         lhsT=ha_w[:, c, g, :].bitcast(FP8X4),
                         lhsT_scale=ha_s[:, c, g, :],
-                        rhs=hb_w[:, g, cols].bitcast(FP8X4),
+                        rhs=hb_w[h][:, g, :].bitcast(FP8X4),
                         rhs_scale=hb_s[:, g, cols],
                         start=(g == 0),
                         stop=(g == GROUPS - 1),
@@ -215,19 +198,48 @@ def tile_list_biaff_none_prior_kernel(
                 )
                 nc.sync.dma_start(out=out[c * CH : (c + 1) * CH, cols], in_=prior[c][:, cols])
 
-        gather_b_scales(0)
-        gather_b_scales(1)
-        load_scales_packed(nc.scalar, ta_s, tab_scales)
-        load_scales_packed(nc.scalar, wa_sraw, wa_scales)
+        nc.vector.memset(tb_s[32:64, :], 0)
+        nc.vector.memset(tb_s[64:128, :], 0)
+        for plane in (b_planes, ta_s, b_late, a_planes):
+            flat = plane[:] if len(plane.shape) == 2 else plane[:].rearrange("p a n -> p (a n)")
+            for first in range(0, flat.shape[1], ZERO_RUN):
+                nc.gpsimd.memset(flat[:, first : first + ZERO_RUN], 0)
+
+        nc.sync.dma_start(list_b[:], offs2)
+        load_rows(nc.sync, tb_s[0:ROWS, :], tab2_scales)
+        load_rows(nc.sync, wb_sraw[:], wb_scales)
+        load_weight(wb_raw[0], wb_words, 0)
+        nc.sync.dma_start(out=tb_w[:], in_=words(tab2_words[0]))
+        load_rows(nc.sync, wa_sraw[:], wa_scales)
+        load_rows(nc.scalar, ta_s[0:ROWS, :], tab_scales)
+
+        gather_b_scales(gb_s, 0)
+        reorder_scales(b_rows[:, 0 : R // 4], wb_sraw[:])
+        nc.vector.tensor_copy(out=b_rows[:, R // 4 :], in_=gb_s[0:ROWS, :].bitcast(I32))
+        spread_rows(b_planes, b_rows)
+        load_weight(wb_raw[1], wb_words, 1)
         reorder_words(wb_w[0], wb_raw[0])
-        reorder_scales(wb_s[:].rearrange("p t a g n -> p (t a g n)"), wb_sraw[:].rearrange("p a n -> p (a n)"))
         gather_b_words(0)
+        nc.sync.dma_start(list_a[:], offs)
+        nc.sync.dma_start(out=ta_w[0][:], in_=words(tab_words[0]))
+        gb_s_late = keep.tile([P, HALF], U8, name="gb_s_late", tag="gb_pair0", align_bytes=256)
+        gather_b_scales(gb_s_late, 1)
+        spread_rows(b_late, gb_s_late[:].bitcast(I32))
         reorder_words(wb_w[1], wb_raw[1])
+        nc.sync.dma_start(out=ta_w[1][:], in_=words(tab_words[1]))
+        load_weight(wa_raw[0], wa_words, 0)
+        load_weight(wa_raw[1], wa_words, 1)
+
         for q in range(J // LOOK):
             if q + 1 < J // LOOK:
                 gather_b_words(q + 1)
             else:
-                reorder_scales(wa_s[:].rearrange("p t g n -> p (t g n)"), wa_sraw[:])
+                reorder_scales(a_rows[:, 0 : R // 4], wa_sraw[:])
+                nc.vector.tensor_copy(ga_s[:], ta_s[:].bitcast(U8).indirect(list_a[:]))
+                nc.vector.tensor_copy(out=a_rows[:, R // 4 :], in_=ga_s[0:ROWS, :].bitcast(I32))
+                spread_rows(a_planes, a_rows)
+                for i in range(M // CH):
+                    nc.sync.dma_start(out=prior[i][:], in_=pr[i * CH : (i + 1) * CH, :])
                 reorder_words(wa_w[0], wa_raw[0])
                 gather_a(0)
                 reorder_words(wa_w[1], wa_raw[1])
@@ -235,6 +247,8 @@ def tile_list_biaff_none_prior_kernel(
                 for c in range(2 * q, 2 * q + 2):
                     layer_b(c, g)
 
+        hb_s = keep.tile([P, GROUPS, J], U8, name="hb_s", tag="wa_raw0", align_bytes=256)
+        ga_rest = keep.tile([P, PASSES, M - LOOK], U32, name="ga_rest", tag="wa_raw1", align_bytes=256)
         for c in range(M // CH + LAG):
             if c % 2 == 0 and c // 2 + 1 < M // LOOK:
                 gather_a(c // 2 + 1)

@@ -28,6 +28,7 @@ HALF = 512
 SCORE_SCALE = 0.03125
 LAG = 2
 ROWS = 32
+SPLIT_STORES = 2
 ZERO_RUN = 256
 
 
@@ -38,8 +39,7 @@ def tile_list_biaff_none_prior_kernel(
     with ExitStack() as ctx:
         keep = ctx.enter_context(tc.tile_pool(name="keep", bufs=1))
         stage = ctx.enter_context(tc.tile_pool(name="stage", bufs=4))
-        psum1 = ctx.enter_context(tc.psum_pool(name="psum1", bufs=4))
-        psum2 = ctx.enter_context(tc.psum_pool(name="psum2", bufs=4))
+        psum = ctx.enter_context(tc.psum_pool(name="psum", bufs=8))
 
         def held(name, shape, dtype):
             return keep.tile(shape, dtype, name=name, align_bytes=256)
@@ -52,19 +52,16 @@ def tile_list_biaff_none_prior_kernel(
         tb_s = held("tb_s", [P, T // 4], I32)
         wa_raw = [held("wa_raw%d" % g, [P, PASSES, HALF], I32) for g in range(GROUPS)]
         wb_raw = [held("wb_raw%d" % g, [P, PASSES, HALF], I32) for g in range(GROUPS)]
-        wa_sraw = held("wa_sraw", [ROWS, R // 4], I32)
+        wa_sraw = held("wa_sraw", [P, R // 4], I32)
+        wa_s = held("wa_s", [P, R // 4], I32)
         wb_sraw = held("wb_sraw", [ROWS, R // 4], I32)
         ga_s = held("ga_s", [P, M], U8)
         gb_s = held("gb_s", [P, HALF], U8)
-        a_rows = held("a_rows", [ROWS, (R + M) // 4], I32)
         b_rows = held("b_rows", [ROWS, (R + HALF) // 4], I32)
-        a_planes = held("a_planes", [P, PASSES, (R + M) // 4], I32)
         b_planes = held("b_planes", [P, PASSES, (R + HALF) // 4], I32)
         b_late = held("b_late", [P, PASSES, HALF // 4], I32)
         wa_w = [held("wa_w%d" % g, [P, PACK, PASSES, P], I32) for g in range(GROUPS)]
         wb_w = [held("wb_w%d" % g, [P, PACK, PASSES, P], I32) for g in range(GROUPS)]
-        ga_first = held("ga_first", [P, PASSES, LOOK], U32)
-        gb_pair = [held("gb_pair%d" % q, [P, LOOK], U32) for q in range(J // LOOK)]
         gb_w = held("gb_w", [P, PASSES, 2 * J], U8)
         hb16 = held("hb16", [P, GROUPS, J, PACK], BF16)
         hb_w = [held("hb_w%d" % h, [P, GROUPS, HALF], U32) for h in range(J // HALF)]
@@ -81,6 +78,14 @@ def tile_list_biaff_none_prior_kernel(
 
         def load_rows(queue, dst, src):
             queue.dma_start(out=dst, in_=src.bitcast(I32).rearrange("a q n -> q a n"))
+
+        def load_packed(dst, src):
+            rows = src.bitcast(I32)
+            for q in range(4):
+                nc.sync.dma_start(out=dst[32 * q : 32 * q + 8, :], in_=rows[:, 4 * q : 4 * q + 4, :])
+
+        def after(slot, name, shape, dtype):
+            return keep.tile(shape, dtype, name=name, tag=slot, align_bytes=256)
 
         def spread_rows(planes, rows):
             for q in range(4):
@@ -107,36 +112,36 @@ def tile_list_biaff_none_prior_kernel(
                 tb_s[:].bitcast(U8).indirect(list_b[:, h * HALF // 16 : (h + 1) * HALF // 16]),
             )
 
-        def gather_b_words(q):
+        def gather_b_words(q, pairs):
             cols = slice(q * LOOK, (q + 1) * LOOK)
-            nc.vector.tensor_copy(gb_pair[q][:], tb_w[:].bitcast(U32).indirect(entries(list_b, q)))
+            nc.vector.tensor_copy(pairs, tb_w[:].bitcast(U32).indirect(entries(list_b, q)))
             nc.vector.tensor_copy(
                 out=gb_w[:].bitcast(U16)[:, :, cols],
-                in_=gb_pair[q][:].bitcast(U16).rearrange("p (n d) -> p d n", d=PASSES),
+                in_=pairs.bitcast(U16).rearrange("p (n d) -> p d n", d=PASSES),
             )
 
-        def ga_cols(a, first, count):
-            if first < LOOK:
-                return ga_first[:, a, first : first + count]
-            return ga_rest[:, a, first - LOOK : first - LOOK + count]
-
-        def gather_a(q):
+        def gather_a(q, slot):
+            picked = after(slot, "ga_w%d" % q, [P, PASSES, LOOK], U32)
             for a in range(PASSES):
-                nc.vector.tensor_copy(ga_cols(a, q * LOOK, LOOK), ta_w[a][:].bitcast(U32).indirect(entries(list_a, q)))
+                nc.vector.tensor_copy(picked[:, a, :], ta_w[a][:].bitcast(U32).indirect(entries(list_a, q)))
+            return picked
 
         def weight_scale(planes, a, t, g):
             first = (t * GROUPS + g) * P // 4
             return planes[:, a, first : first + P // 4].bitcast(U8)
 
+        def interleave(dst, bank):
+            nc.scalar.copy(out=dst, in_=bank[:].rearrange("p (t n) -> p n t", t=PACK))
+
         def layer_b(c, g):
-            bank = psum1.tile([P, PACK, CH], F32, name="layer_bank")
+            bank = psum.tile([P, HALF], F32, name="bank")
             early = c * CH < HALF
             planes = b_planes if early else b_late
             first = (R + c * CH) // 4 if early else (c * CH - HALF) // 4
             for t in range(PACK):
                 for a in range(PASSES):
                     nc.tensor.matmul_mx(
-                        out=bank[:, t, :],
+                        out=bank[:, t * CH : (t + 1) * CH],
                         lhsT=wb_w[g][:, t, a, :].bitcast(FP8X4),
                         lhsT_scale=weight_scale(b_planes, a, t, g),
                         rhs=gb_w[:, a, 2 * c * CH : 2 * (c + 1) * CH].bitcast(FP4X4),
@@ -144,7 +149,7 @@ def tile_list_biaff_none_prior_kernel(
                         start=(a == 0),
                         stop=(a == PASSES - 1),
                     )
-            nc.scalar.copy(out=hb16[:, g, c * CH : (c + 1) * CH, :], in_=bank[:].rearrange("p t n -> p n t"))
+            interleave(hb16[:, g, c * CH : (c + 1) * CH, :], bank)
 
         def quantize_b(h, g):
             cols = slice(h * HALF, (h + 1) * HALF)
@@ -154,22 +159,24 @@ def tile_list_biaff_none_prior_kernel(
                 in_=hb16[:, g, cols, :].rearrange("p n t -> p (n t)"),
             )
 
-        def layer_a(c):
+        def layer_a(c, picked):
             ha16 = stage.tile([P, GROUPS, CH, PACK], BF16, name="ha16", align_bytes=256)
+            first = c * CH % LOOK
             for g in range(GROUPS):
-                bank = psum1.tile([P, PACK, CH], F32, name="layer_bank")
+                bank = psum.tile([P, HALF], F32, name="bank")
                 for t in range(PACK):
+                    word = (t * GROUPS + g) * P // 4
                     for a in range(PASSES):
                         nc.tensor.matmul_mx(
-                            out=bank[:, t, :],
+                            out=bank[:, t * CH : (t + 1) * CH],
                             lhsT=wa_w[g][:, t, a, :].bitcast(FP8X4),
-                            lhsT_scale=weight_scale(a_planes, a, t, g),
-                            rhs=ga_cols(a, c * CH, CH).bitcast(FP8X4),
-                            rhs_scale=a_planes[:, a, (R + c * CH) // 4 : (R + (c + 1) * CH) // 4].bitcast(U8),
+                            lhsT_scale=wa_s[4 * a :, word : word + P // 4].bitcast(U8),
+                            rhs=picked[:, a, first : first + CH].bitcast(FP8X4),
+                            rhs_scale=ga_s[4 * a :, c * CH : (c + 1) * CH],
                             start=(a == 0),
                             stop=(a == PASSES - 1),
                         )
-                nc.scalar.copy(out=ha16[:, g, :, :], in_=bank[:].rearrange("p t n -> p n t"))
+                interleave(ha16[:, g, :, :], bank)
             return ha16
 
         def quantize_a(c, ha16):
@@ -182,7 +189,7 @@ def tile_list_biaff_none_prior_kernel(
         def scores(c):
             for h in range(J // HALF):
                 cols = slice(h * HALF, (h + 1) * HALF)
-                bank = psum2.tile([P, HALF], F32, name="score_bank")
+                bank = psum.tile([P, HALF], F32, name="bank")
                 for g in range(GROUPS):
                     nc.tensor.matmul_mx(
                         out=bank[:],
@@ -196,11 +203,14 @@ def tile_list_biaff_none_prior_kernel(
                 nc.vector.scalar_tensor_tensor(
                     out=prior[c][:, cols], in0=bank[:], scalar=SCORE_SCALE, in1=prior[c][:, cols], op0=MULT, op1=ADD
                 )
-                nc.sync.dma_start(out=out[c * CH : (c + 1) * CH, cols], in_=prior[c][:, cols])
+                if c >= M // CH - SPLIT_STORES:
+                    nc.sync.dma_start(out=out[c * CH : (c + 1) * CH, cols], in_=prior[c][:, cols])
+            if c < M // CH - SPLIT_STORES:
+                nc.sync.dma_start(out=out[c * CH : (c + 1) * CH, :], in_=prior[c][:])
 
         nc.vector.memset(tb_s[32:64, :], 0)
         nc.vector.memset(tb_s[64:128, :], 0)
-        for plane in (b_planes, ta_s, b_late, a_planes):
+        for plane in (b_planes, b_late, ta_s, wa_sraw):
             flat = plane[:] if len(plane.shape) == 2 else plane[:].rearrange("p a n -> p (a n)")
             for first in range(0, flat.shape[1], ZERO_RUN):
                 nc.gpsimd.memset(flat[:, first : first + ZERO_RUN], 0)
@@ -208,52 +218,52 @@ def tile_list_biaff_none_prior_kernel(
         nc.sync.dma_start(list_b[:], offs2)
         load_rows(nc.sync, tb_s[0:ROWS, :], tab2_scales)
         load_rows(nc.sync, wb_sraw[:], wb_scales)
-        load_weight(wb_raw[0], wb_words, 0)
         nc.sync.dma_start(out=tb_w[:], in_=words(tab2_words[0]))
-        load_rows(nc.sync, wa_sraw[:], wa_scales)
-        load_rows(nc.scalar, ta_s[0:ROWS, :], tab_scales)
+        load_weight(wb_raw[0], wb_words, 0)
 
         gather_b_scales(gb_s, 0)
         reorder_scales(b_rows[:, 0 : R // 4], wb_sraw[:])
         nc.vector.tensor_copy(out=b_rows[:, R // 4 :], in_=gb_s[0:ROWS, :].bitcast(I32))
         spread_rows(b_planes, b_rows)
         load_weight(wb_raw[1], wb_words, 1)
-        reorder_words(wb_w[0], wb_raw[0])
-        gather_b_words(0)
         nc.sync.dma_start(list_a[:], offs)
+        load_packed(ta_s, tab_scales)
         nc.sync.dma_start(out=ta_w[0][:], in_=words(tab_words[0]))
-        gb_s_late = keep.tile([P, HALF], U8, name="gb_s_late", tag="gb_pair0", align_bytes=256)
+
+        gather_b_words(0, held("pairs0", [P, LOOK], U32)[:])
+        reorder_words(wb_w[0], wb_raw[0])
+        gather_b_words(1, after("wb_raw0", "pairs1", [P, LOOK], U32)[:])
+        gb_s_late = after("wb_raw0", "gb_s_late", [P, HALF], U8)
         gather_b_scales(gb_s_late, 1)
         spread_rows(b_late, gb_s_late[:].bitcast(I32))
-        reorder_words(wb_w[1], wb_raw[1])
         nc.sync.dma_start(out=ta_w[1][:], in_=words(tab_words[1]))
+        load_packed(wa_sraw, wa_scales)
         load_weight(wa_raw[0], wa_words, 0)
         load_weight(wa_raw[1], wa_words, 1)
+        for i in range(M // CH):
+            nc.sync.dma_start(out=prior[i][:], in_=pr[i * CH : (i + 1) * CH, :])
 
-        for q in range(J // LOOK):
-            if q + 1 < J // LOOK:
-                gather_b_words(q + 1)
-            else:
-                reorder_scales(a_rows[:, 0 : R // 4], wa_sraw[:])
-                nc.vector.tensor_copy(ga_s[:], ta_s[:].bitcast(U8).indirect(list_a[:]))
-                nc.vector.tensor_copy(out=a_rows[:, R // 4 :], in_=ga_s[0:ROWS, :].bitcast(I32))
-                spread_rows(a_planes, a_rows)
-                for i in range(M // CH):
-                    nc.sync.dma_start(out=prior[i][:], in_=pr[i * CH : (i + 1) * CH, :])
-                reorder_words(wa_w[0], wa_raw[0])
-                gather_a(0)
-                reorder_words(wa_w[1], wa_raw[1])
+        reorder_words(wb_w[1], wb_raw[1])
+        pairs_late = after("wb_raw1", "pairs_late", [P, 2, LOOK], U32)
+        gather_b_words(2, pairs_late[:, 0, :])
+        gather_b_words(3, pairs_late[:, 1, :])
+        for h in range(J // HALF):
             for g in range(GROUPS):
-                for c in range(2 * q, 2 * q + 2):
+                for c in range(h * HALF // CH, (h + 1) * HALF // CH):
                     layer_b(c, g)
 
-        hb_s = keep.tile([P, GROUPS, J], U8, name="hb_s", tag="wa_raw0", align_bytes=256)
-        ga_rest = keep.tile([P, PASSES, M - LOOK], U32, name="ga_rest", tag="wa_raw1", align_bytes=256)
+        nc.vector.tensor_copy(ga_s[:], ta_s[:].bitcast(U8).indirect(list_a[:]))
+        picked = [gather_a(0, "picked_even")]
+        reorder_scales(wa_s[:], wa_sraw[:])
+        reorder_words(wa_w[0], wa_raw[0])
+        reorder_words(wa_w[1], wa_raw[1])
+
+        hb_s = after("wa_raw0", "hb_s", [P, GROUPS, J], U8)
         for c in range(M // CH + LAG):
             if c % 2 == 0 and c // 2 + 1 < M // LOOK:
-                gather_a(c // 2 + 1)
+                picked.append(gather_a(c // 2 + 1, "wa_raw1" if c % 4 == 0 else "picked_even"))
             if c < M // CH:
-                ha16 = layer_a(c)
+                ha16 = layer_a(c, picked[c // 2])
             if c == 0:
                 for h in range(J // HALF):
                     for g in range(GROUPS):

@@ -30,6 +30,7 @@ LAG = 2
 ROWS = 32
 SPLIT_STORES = 2
 ZERO_RUN = 256
+WIDE = 3
 
 
 def tile_list_biaff_none_prior_kernel(
@@ -179,11 +180,35 @@ def tile_list_biaff_none_prior_kernel(
                 interleave(ha16[:, g, :, :], bank)
             return ha16
 
+        def layer_a_wide(picked, q):
+            both = stage.tile([P, 2, GROUPS, CH, PACK], BF16, name="both16", align_bytes=256, bufs=2)
+            for g in range(GROUPS):
+                for u in range(2):
+                    bank = psum.tile([P, HALF], F32, name="bank")
+                    for e in range(2):
+                        t = 2 * u + e
+                        word = (t * GROUPS + g) * P // 4
+                        for a in range(PASSES):
+                            nc.tensor.matmul_mx(
+                                out=bank[:, e * LOOK : (e + 1) * LOOK],
+                                lhsT=wa_w[g][:, t, a, :].bitcast(FP8X4),
+                                lhsT_scale=wa_s[4 * a :, word : word + P // 4].bitcast(U8),
+                                rhs=picked[:, a, :].bitcast(FP8X4),
+                                rhs_scale=ga_s[4 * a :, q * LOOK : (q + 1) * LOOK],
+                                start=(a == 0),
+                                stop=(a == PASSES - 1),
+                            )
+                    nc.scalar.copy(
+                        out=both[:, :, g, :, 2 * u : 2 * u + 2],
+                        in_=bank[:].rearrange("p (e c n) -> p c n e", e=2, c=2),
+                    )
+            return both
+
         def quantize_a(c, ha16):
             nc.vector.quantize_mx(
                 out=ha_w[:, c, :, :].rearrange("p g n -> p (g n)").bitcast(FP8X4),
                 scales=ha_s[:, c, :, :].rearrange("p g n -> p (g n)"),
-                in_=ha16[:].rearrange("p g n t -> p (g n t)"),
+                in_=ha16.rearrange("p g n t -> p (g n t)"),
             )
 
         def scores(c):
@@ -259,16 +284,21 @@ def tile_list_biaff_none_prior_kernel(
         reorder_words(wa_w[1], wa_raw[1])
 
         hb_s = after("wa_raw0", "hb_s", [P, GROUPS, J], U8)
-        for c in range(M // CH + LAG):
-            if c % 2 == 0 and c // 2 + 1 < M // LOOK:
-                picked.append(gather_a(c // 2 + 1, "wa_raw1" if c % 4 == 0 else "picked_even"))
-            if c < M // CH:
-                ha16 = layer_a(c, picked[c // 2])
-            if c == 0:
+        for q in range(WIDE):
+            picked.append(gather_a(q + 1, "wa_raw1" if q % 2 == 0 else "picked_even"))
+            both = layer_a_wide(picked[q], q)
+            if q == 0:
                 for h in range(J // HALF):
                     for g in range(GROUPS):
                         quantize_b(h, g)
-            if c >= LAG:
-                scores(c - LAG)
+            else:
+                scores(2 * q - 2)
+                scores(2 * q - 1)
+            quantize_a(2 * q, both[:, 0])
+            quantize_a(2 * q + 1, both[:, 1])
+        for c in range(2 * WIDE, M // CH + LAG):
             if c < M // CH:
-                quantize_a(c, ha16)
+                ha16 = layer_a(c, picked[c // 2])
+            scores(c - LAG)
+            if c < M // CH:
+                quantize_a(c, ha16[:])

@@ -26,11 +26,9 @@ CH = 128
 LOOK = 256
 HALF = 512
 SCORE_SCALE = 0.03125
-LAG = 2
 ROWS = 32
-SPLIT_STORES = 2
+SPLIT_STORES = 3
 ZERO_RUN = 256
-WIDE = 3
 
 
 def tile_list_biaff_none_prior_kernel(
@@ -156,7 +154,7 @@ def tile_list_biaff_none_prior_kernel(
             cols = slice(h * HALF, (h + 1) * HALF)
             nc.vector.quantize_mx(
                 out=hb_w[h][:, g, :].bitcast(FP8X4),
-                scales=hb_s[:, g, cols],
+                scales=hb_s[h][:, g, :],
                 in_=hb16[:, g, cols, :].rearrange("p n t -> p (n t)"),
             )
 
@@ -181,7 +179,7 @@ def tile_list_biaff_none_prior_kernel(
             return ha16
 
         def layer_a_wide(picked, q):
-            both = stage.tile([P, 2, GROUPS, CH, PACK], BF16, name="both16", align_bytes=256, bufs=2)
+            both = held("both16_%d" % q, [P, 2, GROUPS, CH, PACK], BF16)
             for g in range(GROUPS):
                 for u in range(2):
                     bank = psum.tile([P, HALF], F32, name="bank")
@@ -211,8 +209,15 @@ def tile_list_biaff_none_prior_kernel(
                 in_=ha16.rearrange("p g n t -> p (g n t)"),
             )
 
-        def scores(c):
-            for h in range(J // HALF):
+        def quantize_group(c, g, ha16):
+            nc.vector.quantize_mx(
+                out=ha_w[:, c, g, :].bitcast(FP8X4),
+                scales=ha_s[:, c, g, :],
+                in_=ha16[:, g, :, :].rearrange("p n t -> p (n t)"),
+            )
+
+        def scores(c, halves=(0, 1)):
+            for h in halves:
                 cols = slice(h * HALF, (h + 1) * HALF)
                 bank = psum.tile([P, HALF], F32, name="bank")
                 for g in range(GROUPS):
@@ -221,7 +226,7 @@ def tile_list_biaff_none_prior_kernel(
                         lhsT=ha_w[:, c, g, :].bitcast(FP8X4),
                         lhsT_scale=ha_s[:, c, g, :],
                         rhs=hb_w[h][:, g, :].bitcast(FP8X4),
-                        rhs_scale=hb_s[:, g, cols],
+                        rhs_scale=hb_s[h][:, g, :],
                         start=(g == 0),
                         stop=(g == GROUPS - 1),
                     )
@@ -230,7 +235,7 @@ def tile_list_biaff_none_prior_kernel(
                 )
                 if c >= M // CH - SPLIT_STORES:
                     nc.sync.dma_start(out=out[c * CH : (c + 1) * CH, cols], in_=prior[c][:, cols])
-            if c < M // CH - SPLIT_STORES:
+            if c < M // CH - SPLIT_STORES and 1 in halves:
                 nc.sync.dma_start(out=out[c * CH : (c + 1) * CH, :], in_=prior[c][:])
 
         nc.vector.memset(tb_s[32:64, :], 0)
@@ -283,22 +288,39 @@ def tile_list_biaff_none_prior_kernel(
         reorder_words(wa_w[0], wa_raw[0])
         reorder_words(wa_w[1], wa_raw[1])
 
-        hb_s = after("wa_raw0", "hb_s", [P, GROUPS, J], U8)
-        for q in range(WIDE):
-            picked.append(gather_a(q + 1, "wa_raw1" if q % 2 == 0 else "picked_even"))
-            both = layer_a_wide(picked[q], q)
-            if q == 0:
-                for h in range(J // HALF):
-                    for g in range(GROUPS):
-                        quantize_b(h, g)
-            else:
-                scores(2 * q - 2)
-                scores(2 * q - 1)
-            quantize_a(2 * q, both[:, 0])
-            quantize_a(2 * q + 1, both[:, 1])
-        for c in range(2 * WIDE, M // CH + LAG):
-            if c < M // CH:
-                ha16 = layer_a(c, picked[c // 2])
-            scores(c - LAG)
-            if c < M // CH:
-                quantize_a(c, ha16[:])
+        hb_scales = after("wa_raw0", "hb_s", [P, J // HALF, GROUPS, HALF], U8)
+        hb_s = [hb_scales[:, h] for h in range(J // HALF)]
+        made = {}
+        picked.append(gather_a(1, "wa_raw1"))
+        both = layer_a_wide(picked[0], 0)
+        made[0], made[1] = both[:, 0], both[:, 1]
+        quantize_b(0, 0)
+        quantize_b(0, 1)
+        quantize_b(1, 0)
+        quantize_b(1, 1)
+        quantize_a(0, made[0])
+        quantize_a(1, made[1])
+        picked.append(gather_a(2, "picked_even"))
+        both = layer_a_wide(picked[1], 1)
+        made[2], made[3] = both[:, 0], both[:, 1]
+        scores(0)
+        scores(1)
+        picked.append(gather_a(3, "wa_raw1"))
+        quantize_a(2, made[2])
+        quantize_a(3, made[3])
+        both = layer_a_wide(picked[2], 2)
+        made[4], made[5] = both[:, 0], both[:, 1]
+        scores(2)
+        scores(3)
+        quantize_a(4, made[4])
+        quantize_a(5, made[5])
+        made[6] = layer_a(6, picked[3])[:]
+        scores(4)
+        quantize_a(6, made[6])
+        scores(5, (0,))
+        made[7] = layer_a(7, picked[3])[:]
+        quantize_group(7, 0, made[7])
+        scores(5, (1,))
+        quantize_group(7, 1, made[7])
+        scores(6)
+        scores(7)

@@ -178,8 +178,9 @@ def tile_list_biaff_none_prior_kernel(
                 interleave(ha16[:, g, :, :], bank)
             return ha16
 
-        def layer_a_wide(picked, q):
+        def layer_a_wide(picked, q, by_tile=False):
             both = held("both16_%d" % q, [P, 2, GROUPS, CH, PACK], BF16)
+            later = []
             for g in range(GROUPS):
                 for u in range(2):
                     bank = psum.tile([P, HALF], F32, name="bank")
@@ -196,10 +197,15 @@ def tile_list_biaff_none_prior_kernel(
                                 start=(a == 0),
                                 stop=(a == PASSES - 1),
                             )
-                    nc.scalar.copy(
-                        out=both[:, :, g, :, 2 * u : 2 * u + 2],
-                        in_=bank[:].rearrange("p (e c n) -> p c n e", e=2, c=2),
-                    )
+                    dst = both[:, :, g, :, 2 * u : 2 * u + 2]
+                    src = bank[:].rearrange("p (e c n) -> p c n e", e=2, c=2)
+                    if by_tile:
+                        nc.scalar.copy(out=dst[:, 0], in_=src[:, 0])
+                        later.append((dst[:, 1], src[:, 1]))
+                    else:
+                        nc.scalar.copy(out=dst, in_=src)
+            for dst, src in later:
+                nc.scalar.copy(out=dst, in_=src)
             return both
 
         def quantize_a(c, ha16):
@@ -292,7 +298,7 @@ def tile_list_biaff_none_prior_kernel(
         hb_s = [hb_scales[:, h] for h in range(J // HALF)]
         made = {}
         picked.append(gather_a(1, "wa_raw1"))
-        both = layer_a_wide(picked[0], 0)
+        both = layer_a_wide(picked[0], 0, by_tile=True)
         made[0], made[1] = both[:, 0], both[:, 1]
         quantize_b(0, 0)
         quantize_b(0, 1)

@@ -222,22 +222,23 @@ def tile_list_biaff_none_prior_kernel(
                 in_=ha16[:, g, :, :].rearrange("p n t -> p (n t)"),
             )
 
-        def scores(c, halves=(0, 1)):
+        def scores(c, halves=(0, 1), first=0, width=HALF):
             for h in halves:
-                cols = slice(h * HALF, (h + 1) * HALF)
+                cols = slice(h * HALF + first, h * HALF + first + width)
+                inner = slice(first, first + width)
                 bank = psum.tile([P, HALF], F32, name="bank")
                 for g in range(GROUPS):
                     nc.tensor.matmul_mx(
-                        out=bank[:],
+                        out=bank[:, :width],
                         lhsT=ha_w[:, c, g, :].bitcast(FP8X4),
                         lhsT_scale=ha_s[:, c, g, :],
-                        rhs=hb_w[h][:, g, :].bitcast(FP8X4),
-                        rhs_scale=hb_s[h][:, g, :],
+                        rhs=hb_w[h][:, g, inner].bitcast(FP8X4),
+                        rhs_scale=hb_s[h][:, g, inner],
                         start=(g == 0),
                         stop=(g == GROUPS - 1),
                     )
                 nc.vector.scalar_tensor_tensor(
-                    out=prior[c][:, cols], in0=bank[:], scalar=SCORE_SCALE, in1=prior[c][:, cols], op0=MULT, op1=ADD
+                    out=prior[c][:, cols], in0=bank[:, :width], scalar=SCORE_SCALE, in1=prior[c][:, cols], op0=MULT, op1=ADD
                 )
                 if c >= M // CH - SPLIT_STORES:
                     nc.sync.dma_start(out=out[c * CH : (c + 1) * CH, cols], in_=prior[c][:, cols])
@@ -252,13 +253,13 @@ def tile_list_biaff_none_prior_kernel(
                 nc.gpsimd.memset(flat[:, first : first + ZERO_RUN], 0)
 
         nc.sync.dma_start(list_b[:], offs2)
-        load_rows(nc.sync, tb_s[0:ROWS, :], tab2_scales)
         load_rows(nc.sync, wb_sraw[:], wb_scales)
+        load_rows(nc.sync, tb_s[0:ROWS, :], tab2_scales)
         nc.sync.dma_start(out=tb_w[:], in_=words(tab2_words[0]))
         load_weight(wb_raw[0], wb_words, 0)
 
-        gather_b_scales(gb_s, 0)
         reorder_scales(b_rows[:, 0 : R // 4], wb_sraw[:])
+        gather_b_scales(gb_s, 0)
         nc.vector.tensor_copy(out=b_rows[:, R // 4 :], in_=gb_s[0:ROWS, :].bitcast(I32))
         spread_rows(b_planes, b_rows)
         load_weight(wb_raw[1], wb_words, 1)
@@ -329,4 +330,6 @@ def tile_list_biaff_none_prior_kernel(
         scores(5, (1,))
         quantize_group(7, 1, made[7])
         scores(6)
-        scores(7)
+        scores(7, (0,))
+        scores(7, (1,), 0, LOOK)
+        scores(7, (1,), LOOK, LOOK)

@@ -29,6 +29,7 @@ SCORE_SCALE = 0.03125
 ROWS = 32
 SPLIT_STORES = 3
 ZERO_RUN = 256
+WARM = 4
 
 
 def tile_list_biaff_none_prior_kernel(
@@ -50,7 +51,9 @@ def tile_list_biaff_none_prior_kernel(
         tb_w = held("tb_w", [P, T], I32)
         tb_s = held("tb_s", [P, T // 4], I32)
         wa_raw = [held("wa_raw%d" % g, [P, PASSES, HALF], I32) for g in range(GROUPS)]
-        wb_raw = [held("wb_raw%d" % g, [P, PASSES, HALF], I32) for g in range(GROUPS)]
+        wb_head = held("wb_head", [P, PASSES, CH], I32)
+        wb_rest = held("wb_raw0", [P, PASSES, HALF - CH], I32)
+        wb_raw1 = held("wb_raw1", [P, PASSES, HALF], I32)
         wa_sraw = held("wa_sraw", [P, R // 4], I32)
         wa_s = held("wa_s", [P, R // 4], I32)
         wb_sraw = held("wb_sraw", [ROWS, R // 4], I32)
@@ -74,6 +77,17 @@ def tile_list_biaff_none_prior_kernel(
         def load_weight(dst, src, g):
             view = src.rearrange("a p n t -> p a (n t)").bitcast(I32)
             nc.sync.dma_start(out=dst[:], in_=view[:, :, g * HALF : (g + 1) * HALF])
+
+        def load_columns(dst, src, first, last):
+            view = src.rearrange("a p n t -> p a (n t)").bitcast(I32)
+            nc.sync.dma_start(out=dst[:], in_=view[:, :, first:last])
+
+        def reorder_part(dst, raw, first, last):
+            for a in range(PASSES):
+                nc.vector.tensor_copy(
+                    out=dst[:, :, a, first // PACK : last // PACK].rearrange("p t (b i) -> p t b i", i=RUN),
+                    in_=raw[:, a, :].rearrange("p (b t i) -> p t b i", t=PACK, i=RUN),
+                )
 
         def load_rows(queue, dst, src):
             queue.dma_start(out=dst, in_=src.bitcast(I32).rearrange("a q n -> q a n"))
@@ -255,20 +269,34 @@ def tile_list_biaff_none_prior_kernel(
         nc.sync.dma_start(list_b[:], offs2)
         load_rows(nc.sync, wb_sraw[:], wb_scales)
         load_rows(nc.sync, tb_s[0:ROWS, :], tab2_scales)
+        load_columns(wb_head, wb_words, 0, CH)
         nc.sync.dma_start(out=tb_w[:], in_=words(tab2_words[0]))
-        load_weight(wb_raw[0], wb_words, 0)
+        load_columns(wb_rest, wb_words, CH, HALF)
+
+        warm = psum.tile([P, HALF], F32, name="bank")
+        for i in range(WARM):
+            nc.tensor.matmul_mx(
+                out=warm[:],
+                lhsT=wb_head[:, 0, :].bitcast(FP8X4),
+                lhsT_scale=tb_s[:].bitcast(U8)[:, 0:P],
+                rhs=tb_w[:].bitcast(U8)[:, 0 : 2 * HALF].bitcast(FP4X4),
+                rhs_scale=tb_s[:].bitcast(U8)[:, 0:HALF],
+                start=True,
+                stop=True,
+            )
 
         reorder_scales(b_rows[:, 0 : R // 4], wb_sraw[:])
         gather_b_scales(gb_s, 0)
         nc.vector.tensor_copy(out=b_rows[:, R // 4 :], in_=gb_s[0:ROWS, :].bitcast(I32))
         spread_rows(b_planes, b_rows)
-        load_weight(wb_raw[1], wb_words, 1)
+        load_weight(wb_raw1, wb_words, 1)
         nc.sync.dma_start(list_a[:], offs)
         load_packed(ta_s, tab_scales)
         nc.sync.dma_start(out=ta_w[0][:], in_=words(tab_words[0]))
 
+        reorder_part(wb_w[0], wb_head, 0, CH)
         gather_b_words(0, held("pairs0", [P, LOOK], U32)[:])
-        reorder_words(wb_w[0], wb_raw[0])
+        reorder_part(wb_w[0], wb_rest, CH, HALF)
         gather_b_words(1, after("wb_raw0", "pairs1", [P, LOOK], U32)[:])
         gb_s_late = after("wb_raw0", "gb_s_late", [P, HALF], U8)
         gather_b_scales(gb_s_late, 1)
@@ -280,7 +308,7 @@ def tile_list_biaff_none_prior_kernel(
         for i in range(M // CH):
             nc.sync.dma_start(out=prior[i][:], in_=pr[i * CH : (i + 1) * CH, :])
 
-        reorder_words(wb_w[1], wb_raw[1])
+        reorder_words(wb_w[1], wb_raw1)
         pairs_late = after("wb_raw1", "pairs_late", [P, 2, LOOK], U32)
         gather_b_words(2, pairs_late[:, 0, :])
         gather_b_words(3, pairs_late[:, 1, :])

@@ -39,10 +39,14 @@ def tile_list_biaff_none_prior_kernel(
     with ExitStack() as ctx:
         keep = ctx.enter_context(tc.tile_pool(name="keep", bufs=1))
         stage = ctx.enter_context(tc.tile_pool(name="stage", bufs=4))
+        tied = ctx.enter_context(tc.tile_pool(name="tied", bufs=1))
         psum = ctx.enter_context(tc.psum_pool(name="psum", bufs=8))
 
         def held(name, shape, dtype):
             return keep.tile(shape, dtype, name=name, align_bytes=256)
+
+        def placed(name, shape, dtype, kib):
+            return tied.tile(shape, dtype, name=name, align_bytes=256, offset=int(kib * 1024))
 
         list_a = keep.tile([P, M // 16], U16, name="list_a")
         list_b = keep.tile([P, J // 16], U16, name="list_b")
@@ -50,14 +54,14 @@ def tile_list_biaff_none_prior_kernel(
         ta_s = held("ta_s", [P, T // 4], I32)
         tb_w = held("tb_w", [P, T], I32)
         tb_s = held("tb_s", [P, T // 4], I32)
-        wa_raw = [held("wa_raw%d" % g, [P, PASSES, HALF], I32) for g in range(GROUPS)]
+        wa_raw = [held("wa_raw0", [P, PASSES, HALF], I32), placed("wa_raw1", [P, PASSES, HALF], I32, 0)]
         wb_head = held("wb_head", [P, PASSES, CH], I32)
         wb_rest = held("wb_raw0", [P, PASSES, HALF - CH], I32)
         wb_raw1 = held("wb_raw1", [P, PASSES, HALF], I32)
         wa_sraw = held("wa_sraw", [P, R // 4], I32)
         wa_s = held("wa_s", [P, R // 4], I32)
         wb_sraw = held("wb_sraw", [ROWS, R // 4], I32)
-        ga_s = held("ga_s", [P, M], U8)
+        ga_s = {}
         gb_s = held("gb_s", [P, HALF], U8)
         b_rows = held("b_rows", [ROWS, (R + HALF) // 4], I32)
         b_planes = held("b_planes", [P, PASSES, (R + HALF) // 4], I32)
@@ -133,8 +137,9 @@ def tile_list_biaff_none_prior_kernel(
                 in_=pairs.bitcast(U16).rearrange("p (n d) -> p d n", d=PASSES),
             )
 
-        def gather_a(q, slot):
-            picked = after(slot, "ga_w%d" % q, [P, PASSES, LOOK], U32)
+        def gather_a(q, words_at, scales_at):
+            ga_s[q] = ga_all[:, q * LOOK : (q + 1) * LOOK]
+            picked = placed("ga_w%d" % q, [P, PASSES, LOOK], U32, words_at)
             for a in range(PASSES):
                 nc.vector.tensor_copy(picked[:, a, :], ta_w[a][:].bitcast(U32).indirect(entries(list_a, q)))
             return picked
@@ -168,12 +173,12 @@ def tile_list_biaff_none_prior_kernel(
             cols = slice(h * HALF, (h + 1) * HALF)
             nc.vector.quantize_mx(
                 out=hb_w[h][:, g, :].bitcast(FP8X4),
-                scales=hb_s[h][:, g, :],
+                scales=hb_s[h, g][:],
                 in_=hb16[:, g, cols, :].rearrange("p n t -> p (n t)"),
             )
 
-        def layer_a(c, picked):
-            ha16 = stage.tile([P, GROUPS, CH, PACK], BF16, name="ha16", align_bytes=256)
+        def layer_a(c, picked, kib):
+            ha16 = placed("ha16_%d" % c, [P, GROUPS, CH, PACK], BF16, kib)
             first = c * CH % LOOK
             for g in range(GROUPS):
                 bank = psum.tile([P, HALF], F32, name="bank")
@@ -185,7 +190,7 @@ def tile_list_biaff_none_prior_kernel(
                             lhsT=wa_w[g][:, t, a, :].bitcast(FP8X4),
                             lhsT_scale=wa_s[4 * a :, word : word + P // 4].bitcast(U8),
                             rhs=picked[:, a, first : first + CH].bitcast(FP8X4),
-                            rhs_scale=ga_s[4 * a :, c * CH : (c + 1) * CH],
+                            rhs_scale=ga_s[c * CH // LOOK][4 * a :, first : first + CH],
                             start=(a == 0),
                             stop=(a == PASSES - 1),
                         )
@@ -193,7 +198,12 @@ def tile_list_biaff_none_prior_kernel(
             return ha16
 
         def layer_a_wide(picked, q, by_tile=False):
-            both = held("both16_%d" % q, [P, 2, GROUPS, CH, PACK], BF16)
+            if by_tile:
+                tiles = [placed("ha16_%d" % c, [P, GROUPS, CH, PACK], BF16, 8 + 2 * c) for c in range(2)]
+                both = None
+            else:
+                both = placed("both16_%d" % q, [P, 2, GROUPS, CH, PACK], BF16, 8 + 4 * q)
+                tiles = [both[:, 0], both[:, 1]]
             later = []
             for g in range(GROUPS):
                 for u in range(2):
@@ -207,20 +217,19 @@ def tile_list_biaff_none_prior_kernel(
                                 lhsT=wa_w[g][:, t, a, :].bitcast(FP8X4),
                                 lhsT_scale=wa_s[4 * a :, word : word + P // 4].bitcast(U8),
                                 rhs=picked[:, a, :].bitcast(FP8X4),
-                                rhs_scale=ga_s[4 * a :, q * LOOK : (q + 1) * LOOK],
+                                rhs_scale=ga_s[q][4 * a :, :],
                                 start=(a == 0),
                                 stop=(a == PASSES - 1),
                             )
-                    dst = both[:, :, g, :, 2 * u : 2 * u + 2]
                     src = bank[:].rearrange("p (e c n) -> p c n e", e=2, c=2)
                     if by_tile:
-                        nc.scalar.copy(out=dst[:, 0], in_=src[:, 0])
-                        later.append((dst[:, 1], src[:, 1]))
+                        nc.scalar.copy(out=tiles[0][:, g, :, 2 * u : 2 * u + 2], in_=src[:, 0])
+                        later.append((tiles[1][:, g, :, 2 * u : 2 * u + 2], src[:, 1]))
                     else:
-                        nc.scalar.copy(out=dst, in_=src)
+                        nc.scalar.copy(out=both[:, :, g, :, 2 * u : 2 * u + 2], in_=src)
             for dst, src in later:
                 nc.scalar.copy(out=dst, in_=src)
-            return both
+            return tiles[0][:], tiles[1][:]
 
         def quantize_a(c, ha16):
             nc.vector.quantize_mx(
@@ -247,7 +256,7 @@ def tile_list_biaff_none_prior_kernel(
                         lhsT=ha_w[:, c, g, :].bitcast(FP8X4),
                         lhsT_scale=ha_s[:, c, g, :],
                         rhs=hb_w[h][:, g, inner].bitcast(FP8X4),
-                        rhs_scale=hb_s[h][:, g, inner],
+                        rhs_scale=hb_s[h, g][:, inner],
                         start=(g == 0),
                         stop=(g == GROUPS - 1),
                     )
@@ -289,6 +298,8 @@ def tile_list_biaff_none_prior_kernel(
         gather_b_scales(gb_s, 0)
         nc.vector.tensor_copy(out=b_rows[:, R // 4 :], in_=gb_s[0:ROWS, :].bitcast(I32))
         spread_rows(b_planes, b_rows)
+        gb_s_late = after("gb_s", "gb_s_late", [P, HALF], U8)
+        gather_b_scales(gb_s_late, 1)
         load_weight(wb_raw1, wb_words, 1)
         nc.sync.dma_start(list_a[:], offs)
         load_packed(ta_s, tab_scales)
@@ -298,8 +309,6 @@ def tile_list_biaff_none_prior_kernel(
         gather_b_words(0, held("pairs0", [P, LOOK], U32)[:])
         reorder_part(wb_w[0], wb_rest, CH, HALF)
         gather_b_words(1, after("wb_raw0", "pairs1", [P, LOOK], U32)[:])
-        gb_s_late = after("wb_raw0", "gb_s_late", [P, HALF], U8)
-        gather_b_scales(gb_s_late, 1)
         spread_rows(b_late, gb_s_late[:].bitcast(I32))
         nc.sync.dma_start(out=ta_w[1][:], in_=words(tab_words[1]))
         load_packed(wa_sraw, wa_scales)
@@ -317,43 +326,43 @@ def tile_list_biaff_none_prior_kernel(
                 for c in range(h * HALF // CH, (h + 1) * HALF // CH):
                     layer_b(c, g)
 
-        nc.vector.tensor_copy(ga_s[:], ta_s[:].bitcast(U8).indirect(list_a[:]))
-        picked = [gather_a(0, "picked_even")]
+        ga_all = held("ga_all", [P, M], U8)
+        nc.vector.tensor_copy(ga_all[:], ta_s[:].bitcast(U8).indirect(list_a[:]))
+        picked = [gather_a(0, 4, 6)]
         reorder_scales(wa_s[:], wa_sraw[:])
         reorder_words(wa_w[0], wa_raw[0])
         reorder_words(wa_w[1], wa_raw[1])
 
-        hb_scales = after("wa_raw0", "hb_s", [P, J // HALF, GROUPS, HALF], U8)
-        hb_s = [hb_scales[:, h] for h in range(J // HALF)]
+        hb_s = {}
+        for h, g, at in ((0, 0, 24), (0, 1, 2.5), (1, 0, 3), (1, 1, 3.5)):
+            hb_s[h, g] = placed("hb_s%d%d" % (h, g), [P, HALF], U8, at)
         made = {}
-        picked.append(gather_a(1, "wa_raw1"))
-        both = layer_a_wide(picked[0], 0, by_tile=True)
-        made[0], made[1] = both[:, 0], both[:, 1]
+        picked.append(gather_a(1, 0, 2))
+        made[0] = layer_a(0, picked[0], 8)[:]
+        made[1] = layer_a(1, picked[0], 10)[:]
         quantize_b(0, 0)
         quantize_b(0, 1)
         quantize_b(1, 0)
         quantize_b(1, 1)
         quantize_a(0, made[0])
+        picked.append(gather_a(2, 8, 6))
         quantize_a(1, made[1])
-        picked.append(gather_a(2, "picked_even"))
-        both = layer_a_wide(picked[1], 1)
-        made[2], made[3] = both[:, 0], both[:, 1]
+        made[2], made[3] = layer_a_wide(picked[1], 1)
         scores(0)
         scores(1)
-        picked.append(gather_a(3, "wa_raw1"))
         quantize_a(2, made[2])
         quantize_a(3, made[3])
-        both = layer_a_wide(picked[2], 2)
-        made[4], made[5] = both[:, 0], both[:, 1]
+        picked.append(gather_a(3, 12, 14))
+        made[4], made[5] = layer_a_wide(picked[2], 2)
         scores(2)
         scores(3)
         quantize_a(4, made[4])
         quantize_a(5, made[5])
-        made[6] = layer_a(6, picked[3])[:]
+        made[6] = layer_a(6, picked[3], 20)[:]
         scores(4)
         quantize_a(6, made[6])
         scores(5, (0,))
-        made[7] = layer_a(7, picked[3])[:]
+        made[7] = layer_a(7, picked[3], 22)[:]
         quantize_group(7, 0, made[7])
         scores(5, (1,))
         quantize_group(7, 1, made[7])

@@ -28,8 +28,9 @@ HALF = 512
 SCORE_SCALE = 0.03125
 ROWS = 32
 SPLIT_STORES = 3
-ZERO_RUN = 256
-WARM = 4
+WARM = 7
+BANKS = 8
+BANK_BYTES = 2048
 
 
 def tile_list_biaff_none_prior_kernel(
@@ -38,15 +39,17 @@ def tile_list_biaff_none_prior_kernel(
     nc = tc.nc
     with ExitStack() as ctx:
         keep = ctx.enter_context(tc.tile_pool(name="keep", bufs=1))
-        stage = ctx.enter_context(tc.tile_pool(name="stage", bufs=4))
         tied = ctx.enter_context(tc.tile_pool(name="tied", bufs=1))
-        psum = ctx.enter_context(tc.psum_pool(name="psum", bufs=8))
+        psum = ctx.enter_context(tc.psum_pool(name="psum", bufs=1))
 
         def held(name, shape, dtype):
             return keep.tile(shape, dtype, name=name, align_bytes=256)
 
         def placed(name, shape, dtype, kib):
             return tied.tile(shape, dtype, name=name, align_bytes=256, offset=int(kib * 1024))
+
+        def bank_at(name, n):
+            return psum.tile([P, HALF], F32, name=name, offset=n * BANK_BYTES)
 
         list_a = keep.tile([P, M // 16], U16, name="list_a")
         list_b = keep.tile([P, J // 16], U16, name="list_b")
@@ -55,21 +58,23 @@ def tile_list_biaff_none_prior_kernel(
         tb_w = held("tb_w", [P, T], I32)
         tb_s = held("tb_s", [P, T // 4], I32)
         wa_raw = [held("wa_raw0", [P, PASSES, HALF], I32), placed("wa_raw1", [P, PASSES, HALF], I32, 0)]
-        wb_head = held("wb_head", [P, PASSES, CH], I32)
-        wb_rest = held("wb_raw0", [P, PASSES, HALF - CH], I32)
-        wb_raw1 = held("wb_raw1", [P, PASSES, HALF], I32)
+        wb_raw0 = [placed("wb_raw0%d" % a, [P, HALF], I32, 42 + 2 * a) for a in range(PASSES)]
+        wb_raw1 = placed("wb_raw1", [P, PASSES, HALF], I32, 46)
         wa_sraw = held("wa_sraw", [P, R // 4], I32)
         wa_s = held("wa_s", [P, R // 4], I32)
         wb_sraw = held("wb_sraw", [ROWS, R // 4], I32)
-        ga_s = {}
         gb_s = held("gb_s", [P, HALF], U8)
         b_rows = held("b_rows", [ROWS, (R + HALF) // 4], I32)
         b_planes = held("b_planes", [P, PASSES, (R + HALF) // 4], I32)
         b_late = held("b_late", [P, PASSES, HALF // 4], I32)
         wa_w = [held("wa_w%d" % g, [P, PACK, PASSES, P], I32) for g in range(GROUPS)]
         wb_w = [held("wb_w%d" % g, [P, PACK, PASSES, P], I32) for g in range(GROUPS)]
-        gb_w = held("gb_w", [P, PASSES, 2 * J], U8)
-        hb16 = held("hb16", [P, GROUPS, J, PACK], BF16)
+        gb_w = {}
+        hb16 = {
+            (h, g): placed("hb16_%d%d" % (h, g), [P, HALF, PACK], BF16, 26 + 8 * h + 4 * g)
+            for h in range(J // HALF)
+            for g in range(GROUPS)
+        }
         hb_w = [held("hb_w%d" % h, [P, GROUPS, HALF], U32) for h in range(J // HALF)]
         ha_w = held("ha_w", [P, M // CH, GROUPS, CH], U32)
         ha_s = held("ha_s", [P, M // CH, GROUPS, CH], U8)
@@ -82,16 +87,11 @@ def tile_list_biaff_none_prior_kernel(
             view = src.rearrange("a p n t -> p a (n t)").bitcast(I32)
             nc.sync.dma_start(out=dst[:], in_=view[:, :, g * HALF : (g + 1) * HALF])
 
-        def load_columns(dst, src, first, last):
-            view = src.rearrange("a p n t -> p a (n t)").bitcast(I32)
-            nc.sync.dma_start(out=dst[:], in_=view[:, :, first:last])
-
-        def reorder_part(dst, raw, first, last):
-            for a in range(PASSES):
-                nc.vector.tensor_copy(
-                    out=dst[:, :, a, first // PACK : last // PACK].rearrange("p t (b i) -> p t b i", i=RUN),
-                    in_=raw[:, a, :].rearrange("p (b t i) -> p t b i", t=PACK, i=RUN),
-                )
+        def reorder_pass(dst, raw):
+            nc.vector.tensor_copy(
+                out=dst.rearrange("p t (b i) -> p t b i", i=RUN),
+                in_=raw.rearrange("p (b t i) -> p t b i", t=PACK, i=RUN),
+            )
 
         def load_rows(queue, dst, src):
             queue.dma_start(out=dst, in_=src.bitcast(I32).rearrange("a q n -> q a n"))
@@ -123,25 +123,23 @@ def tile_list_biaff_none_prior_kernel(
         def entries(lst, q):
             return lst[:, q * LOOK // 16 : (q + 1) * LOOK // 16]
 
-        def gather_b_scales(dst, h):
-            nc.vector.tensor_copy(
-                dst[:],
-                tb_s[:].bitcast(U8).indirect(list_b[:, h * HALF // 16 : (h + 1) * HALF // 16]),
-            )
+        def gather_b_scales(dst, first, count):
+            nc.vector.tensor_copy(dst[:], tb_s[:].bitcast(U8).indirect(list_b[:, first // 16 : (first + count) // 16]))
 
         def gather_b_words(q, pairs):
-            cols = slice(q * LOOK, (q + 1) * LOOK)
             nc.vector.tensor_copy(pairs, tb_w[:].bitcast(U32).indirect(entries(list_b, q)))
+
+        def part(dst, pairs, c):
             nc.vector.tensor_copy(
-                out=gb_w[:].bitcast(U16)[:, :, cols],
+                out=dst[:].bitcast(U16),
                 in_=pairs.bitcast(U16).rearrange("p (n d) -> p d n", d=PASSES),
             )
+            for i in range(dst.shape[2] // (2 * CH)):
+                gb_w[c + i] = dst[:, :, 2 * i * CH : 2 * (i + 1) * CH]
 
-        def gather_a(q, words_at, scales_at):
-            ga_s[q] = ga_all[:, q * LOOK : (q + 1) * LOOK]
-            picked = placed("ga_w%d" % q, [P, PASSES, LOOK], U32, words_at)
-            for a in range(PASSES):
-                nc.vector.tensor_copy(picked[:, a, :], ta_w[a][:].bitcast(U32).indirect(entries(list_a, q)))
+        def gather_a(q, a, kib):
+            picked = placed("ga_w%d%d" % (q, a), [P, LOOK], U32, kib)
+            nc.vector.tensor_copy(picked[:], ta_w[a][:].bitcast(U32).indirect(entries(list_a, q)))
             return picked
 
         def weight_scale(planes, a, t, g):
@@ -151,8 +149,8 @@ def tile_list_biaff_none_prior_kernel(
         def interleave(dst, bank):
             nc.scalar.copy(out=dst, in_=bank[:].rearrange("p (t n) -> p n t", t=PACK))
 
-        def layer_b(c, g):
-            bank = psum.tile([P, HALF], F32, name="bank")
+        def layer_b(c, g, n):
+            bank = bank_at("bank_b%d%d" % (c, g), n)
             early = c * CH < HALF
             planes = b_planes if early else b_late
             first = (R + c * CH) // 4 if early else (c * CH - HALF) // 4
@@ -162,52 +160,43 @@ def tile_list_biaff_none_prior_kernel(
                         out=bank[:, t * CH : (t + 1) * CH],
                         lhsT=wb_w[g][:, t, a, :].bitcast(FP8X4),
                         lhsT_scale=weight_scale(b_planes, a, t, g),
-                        rhs=gb_w[:, a, 2 * c * CH : 2 * (c + 1) * CH].bitcast(FP4X4),
+                        rhs=gb_w[c][:, a, :].bitcast(FP4X4),
                         rhs_scale=planes[:, a, first : first + CH // 4].bitcast(U8),
                         start=(a == 0),
                         stop=(a == PASSES - 1),
                     )
-            interleave(hb16[:, g, c * CH : (c + 1) * CH, :], bank)
+            inner = c * CH % HALF
+            interleave(hb16[c * CH // HALF, g][:, inner : inner + CH, :], bank)
 
         def quantize_b(h, g):
-            cols = slice(h * HALF, (h + 1) * HALF)
             nc.vector.quantize_mx(
                 out=hb_w[h][:, g, :].bitcast(FP8X4),
                 scales=hb_s[h, g][:],
-                in_=hb16[:, g, cols, :].rearrange("p n t -> p (n t)"),
+                in_=hb16[h, g][:].rearrange("p n t -> p (n t)"),
             )
 
-        def layer_a(c, picked, kib):
-            ha16 = placed("ha16_%d" % c, [P, GROUPS, CH, PACK], BF16, kib)
+        def layer_a(c, g, picked, ha16, n):
             first = c * CH % LOOK
-            for g in range(GROUPS):
-                bank = psum.tile([P, HALF], F32, name="bank")
-                for t in range(PACK):
-                    word = (t * GROUPS + g) * P // 4
-                    for a in range(PASSES):
-                        nc.tensor.matmul_mx(
-                            out=bank[:, t * CH : (t + 1) * CH],
-                            lhsT=wa_w[g][:, t, a, :].bitcast(FP8X4),
-                            lhsT_scale=wa_s[4 * a :, word : word + P // 4].bitcast(U8),
-                            rhs=picked[:, a, first : first + CH].bitcast(FP8X4),
-                            rhs_scale=ga_s[c * CH // LOOK][4 * a :, first : first + CH],
-                            start=(a == 0),
-                            stop=(a == PASSES - 1),
-                        )
-                interleave(ha16[:, g, :, :], bank)
-            return ha16
+            bank = bank_at("bank_a%d%d" % (c, g), n)
+            for t in range(PACK):
+                word = (t * GROUPS + g) * P // 4
+                for a in range(PASSES):
+                    nc.tensor.matmul_mx(
+                        out=bank[:, t * CH : (t + 1) * CH],
+                        lhsT=wa_w[g][:, t, a, :].bitcast(FP8X4),
+                        lhsT_scale=wa_s[4 * a :, word : word + P // 4].bitcast(U8),
+                        rhs=picked[a][:, first : first + CH].bitcast(FP8X4),
+                        rhs_scale=ga_all[4 * a :, c * CH : (c + 1) * CH],
+                        start=(a == 0),
+                        stop=(a == PASSES - 1),
+                    )
+            interleave(ha16[:, g, :, :], bank)
 
-        def layer_a_wide(picked, q, by_tile=False):
-            if by_tile:
-                tiles = [placed("ha16_%d" % c, [P, GROUPS, CH, PACK], BF16, 8 + 2 * c) for c in range(2)]
-                both = None
-            else:
-                both = placed("both16_%d" % q, [P, 2, GROUPS, CH, PACK], BF16, 8 + 4 * q)
-                tiles = [both[:, 0], both[:, 1]]
-            later = []
+        def layer_a_wide(picked, q, n):
+            both = placed("both16_%d" % q, [P, 2, GROUPS, CH, PACK], BF16, 8 + 4 * q)
             for g in range(GROUPS):
                 for u in range(2):
-                    bank = psum.tile([P, HALF], F32, name="bank")
+                    bank = bank_at("bank_w%d%d%d" % (q, g, u), n + 2 * g + u)
                     for e in range(2):
                         t = 2 * u + e
                         word = (t * GROUPS + g) * P // 4
@@ -216,20 +205,14 @@ def tile_list_biaff_none_prior_kernel(
                                 out=bank[:, e * LOOK : (e + 1) * LOOK],
                                 lhsT=wa_w[g][:, t, a, :].bitcast(FP8X4),
                                 lhsT_scale=wa_s[4 * a :, word : word + P // 4].bitcast(U8),
-                                rhs=picked[:, a, :].bitcast(FP8X4),
-                                rhs_scale=ga_s[q][4 * a :, :],
+                                rhs=picked[a][:].bitcast(FP8X4),
+                                rhs_scale=ga_all[4 * a :, q * LOOK : (q + 1) * LOOK],
                                 start=(a == 0),
                                 stop=(a == PASSES - 1),
                             )
                     src = bank[:].rearrange("p (e c n) -> p c n e", e=2, c=2)
-                    if by_tile:
-                        nc.scalar.copy(out=tiles[0][:, g, :, 2 * u : 2 * u + 2], in_=src[:, 0])
-                        later.append((tiles[1][:, g, :, 2 * u : 2 * u + 2], src[:, 1]))
-                    else:
-                        nc.scalar.copy(out=both[:, :, g, :, 2 * u : 2 * u + 2], in_=src)
-            for dst, src in later:
-                nc.scalar.copy(out=dst, in_=src)
-            return tiles[0][:], tiles[1][:]
+                    nc.scalar.copy(out=both[:, :, g, :, 2 * u : 2 * u + 2], in_=src)
+            return both[:, 0], both[:, 1]
 
         def quantize_a(c, ha16):
             nc.vector.quantize_mx(
@@ -245,70 +228,81 @@ def tile_list_biaff_none_prior_kernel(
                 in_=ha16[:, g, :, :].rearrange("p n t -> p (n t)"),
             )
 
-        def scores(c, halves=(0, 1), first=0, width=HALF):
+        def scores(c, n, halves=(0, 1), pieces=1):
             for h in halves:
-                cols = slice(h * HALF + first, h * HALF + first + width)
-                inner = slice(first, first + width)
-                bank = psum.tile([P, HALF], F32, name="bank")
+                bank = bank_at("bank_s%d%d%d" % (c, h, 0), n + h - halves[0])
                 for g in range(GROUPS):
                     nc.tensor.matmul_mx(
-                        out=bank[:, :width],
+                        out=bank[:],
                         lhsT=ha_w[:, c, g, :].bitcast(FP8X4),
                         lhsT_scale=ha_s[:, c, g, :],
-                        rhs=hb_w[h][:, g, inner].bitcast(FP8X4),
-                        rhs_scale=hb_s[h, g][:, inner],
+                        rhs=hb_w[h][:, g, :].bitcast(FP8X4),
+                        rhs_scale=hb_s[h, g][:],
                         start=(g == 0),
                         stop=(g == GROUPS - 1),
                     )
-                nc.vector.scalar_tensor_tensor(
-                    out=prior[c][:, cols], in0=bank[:, :width], scalar=SCORE_SCALE, in1=prior[c][:, cols], op0=MULT, op1=ADD
-                )
-                if c >= M // CH - SPLIT_STORES:
-                    nc.sync.dma_start(out=out[c * CH : (c + 1) * CH, cols], in_=prior[c][:, cols])
+                width = HALF // pieces
+                for first in range(0, HALF, width):
+                    cols = slice(h * HALF + first, h * HALF + first + width)
+                    nc.vector.scalar_tensor_tensor(
+                        out=prior[c][:, cols],
+                        in0=bank[:, first : first + width],
+                        scalar=SCORE_SCALE,
+                        in1=prior[c][:, cols],
+                        op0=MULT,
+                        op1=ADD,
+                    )
+                    if c >= M // CH - SPLIT_STORES:
+                        nc.sync.dma_start(out=out[c * CH : (c + 1) * CH, cols], in_=prior[c][:, cols])
             if c < M // CH - SPLIT_STORES and 1 in halves:
                 nc.sync.dma_start(out=out[c * CH : (c + 1) * CH, :], in_=prior[c][:])
 
-        nc.vector.memset(tb_s[32:64, :], 0)
-        nc.vector.memset(tb_s[64:128, :], 0)
-        for plane in (b_planes, b_late, ta_s, wa_sraw):
-            flat = plane[:] if len(plane.shape) == 2 else plane[:].rearrange("p a n -> p (a n)")
-            for first in range(0, flat.shape[1], ZERO_RUN):
-                nc.gpsimd.memset(flat[:, first : first + ZERO_RUN], 0)
+        nc.gpsimd.memset(tb_s[32:64, :], 0)
+        nc.gpsimd.memset(tb_s[64:128, :], 0)
+        for plane in (wa_sraw, b_planes, b_late, ta_s):
+            nc.vector.memset(plane[:], 0)
 
         nc.sync.dma_start(list_b[:], offs2)
         load_rows(nc.sync, wb_sraw[:], wb_scales)
         load_rows(nc.sync, tb_s[0:ROWS, :], tab2_scales)
-        load_columns(wb_head, wb_words, 0, CH)
+        nc.sync.dma_start(out=wb_raw0[0][:], in_=words(wb_words[0])[:, 0:HALF])
         nc.sync.dma_start(out=tb_w[:], in_=words(tab2_words[0]))
-        load_columns(wb_rest, wb_words, CH, HALF)
+        nc.sync.dma_start(out=wb_raw0[1][:], in_=words(wb_words[1])[:, 0:HALF])
 
-        warm = psum.tile([P, HALF], F32, name="bank")
+        warm = bank_at("warm", BANKS - 1)
         for i in range(WARM):
             nc.tensor.matmul_mx(
                 out=warm[:],
-                lhsT=wb_head[:, 0, :].bitcast(FP8X4),
-                lhsT_scale=tb_s[:].bitcast(U8)[:, 0:P],
-                rhs=tb_w[:].bitcast(U8)[:, 0 : 2 * HALF].bitcast(FP4X4),
-                rhs_scale=tb_s[:].bitcast(U8)[:, 0:HALF],
+                lhsT=wb_raw0[0][:, 0:P].bitcast(FP8X4),
+                lhsT_scale=wa_sraw[:].bitcast(U8)[:, 0:P],
+                rhs=wb_raw0[0][:].bitcast(FP8X4),
+                rhs_scale=wa_sraw[:].bitcast(U8)[:, 0:HALF],
                 start=True,
                 stop=True,
             )
 
         reorder_scales(b_rows[:, 0 : R // 4], wb_sraw[:])
-        gather_b_scales(gb_s, 0)
+        gather_b_scales(gb_s, 0, HALF)
         nc.vector.tensor_copy(out=b_rows[:, R // 4 :], in_=gb_s[0:ROWS, :].bitcast(I32))
         spread_rows(b_planes, b_rows)
         gb_s_late = after("gb_s", "gb_s_late", [P, HALF], U8)
-        gather_b_scales(gb_s_late, 1)
+        gather_b_scales(gb_s_late, HALF, HALF)
         load_weight(wb_raw1, wb_words, 1)
         nc.sync.dma_start(list_a[:], offs)
         load_packed(ta_s, tab_scales)
         nc.sync.dma_start(out=ta_w[0][:], in_=words(tab_words[0]))
 
-        reorder_part(wb_w[0], wb_head, 0, CH)
-        gather_b_words(0, held("pairs0", [P, LOOK], U32)[:])
-        reorder_part(wb_w[0], wb_rest, CH, HALF)
-        gather_b_words(1, after("wb_raw0", "pairs1", [P, LOOK], U32)[:])
+        pairs = held("pairs0", [P, LOOK], U32)
+        gather_b_words(0, pairs[:])
+        for a in range(PASSES):
+            reorder_pass(wb_w[0][:, :, a, :], wb_raw0[a][:])
+        part(placed("gb_w0", [P, PASSES, 2 * CH], U8, 44), pairs[:, :CH], 0)
+        part(placed("gb_w1", [P, PASSES, 2 * CH], U8, 44.5), pairs[:, CH:], 1)
+        pairs = placed("pairs1", [P, LOOK], U32, 45)
+        gather_b_words(1, pairs[:])
+        part(held("gb_w2", [P, PASSES, 2 * CH], U8), pairs[:, :CH], 2)
+        part(held("gb_w3", [P, PASSES, 2 * CH], U8), pairs[:, CH:], 3)
+        reorder_words(wb_w[1], wb_raw1)
         spread_rows(b_late, gb_s_late[:].bitcast(I32))
         nc.sync.dma_start(out=ta_w[1][:], in_=words(tab_words[1]))
         load_packed(wa_sraw, wa_scales)
@@ -317,18 +311,18 @@ def tile_list_biaff_none_prior_kernel(
         for i in range(M // CH):
             nc.sync.dma_start(out=prior[i][:], in_=pr[i * CH : (i + 1) * CH, :])
 
-        reorder_words(wb_w[1], wb_raw1)
-        pairs_late = after("wb_raw1", "pairs_late", [P, 2, LOOK], U32)
-        gather_b_words(2, pairs_late[:, 0, :])
-        gather_b_words(3, pairs_late[:, 1, :])
+        for q in (2, 3):
+            pairs = placed("pairs%d" % q, [P, LOOK], U32, 45 + q)
+            gather_b_words(q, pairs[:])
+            part(held("gb_w%d" % (2 * q), [P, PASSES, 2 * LOOK], U8), pairs[:], 2 * q)
         for h in range(J // HALF):
             for g in range(GROUPS):
                 for c in range(h * HALF // CH, (h + 1) * HALF // CH):
-                    layer_b(c, g)
+                    layer_b(c, g, (g * HALF // CH + c) % BANKS if h == 0 else (g * HALF // CH + c - HALF // CH) % BANKS)
 
         ga_all = held("ga_all", [P, M], U8)
         nc.vector.tensor_copy(ga_all[:], ta_s[:].bitcast(U8).indirect(list_a[:]))
-        picked = [gather_a(0, 4, 6)]
+        picked = [[gather_a(0, a, 4 + a) for a in range(PASSES)]]
         reorder_scales(wa_s[:], wa_sraw[:])
         reorder_words(wa_w[0], wa_raw[0])
         reorder_words(wa_w[1], wa_raw[1])
@@ -337,36 +331,43 @@ def tile_list_biaff_none_prior_kernel(
         for h, g, at in ((0, 0, 24), (0, 1, 2.5), (1, 0, 3), (1, 1, 3.5)):
             hb_s[h, g] = placed("hb_s%d%d" % (h, g), [P, HALF], U8, at)
         made = {}
-        picked.append(gather_a(1, 0, 2))
-        made[0] = layer_a(0, picked[0], 8)[:]
-        made[1] = layer_a(1, picked[0], 10)[:]
+        picked.append([gather_a(1, a, a) for a in range(PASSES)])
+        for c, kib in ((0, 8), (1, 10), (6, 20), (7, 22)):
+            made[c] = placed("ha16_%d" % c, [P, GROUPS, CH, PACK], BF16, kib)[:]
+        for g in range(GROUPS):
+            for c in range(2):
+                layer_a(c, g, picked[0], made[c], 2 * g + c)
         quantize_b(0, 0)
         quantize_b(0, 1)
         quantize_b(1, 0)
+        early = gather_a(2, 0, 34)
         quantize_b(1, 1)
         quantize_a(0, made[0])
-        picked.append(gather_a(2, 8, 6))
         quantize_a(1, made[1])
-        made[2], made[3] = layer_a_wide(picked[1], 1)
-        scores(0)
-        scores(1)
+        picked.append([early, gather_a(2, 1, 10)])
+        made[2], made[3] = layer_a_wide(picked[1], 1, 4)
+        scores(0, 0)
+        scores(1, 2)
         quantize_a(2, made[2])
         quantize_a(3, made[3])
-        picked.append(gather_a(3, 12, 14))
-        made[4], made[5] = layer_a_wide(picked[2], 2)
-        scores(2)
-        scores(3)
+        picked.append([gather_a(3, a, 14 + a) for a in range(PASSES)])
+        made[4], made[5] = layer_a_wide(picked[2], 2, 4)
+        scores(2, 0)
+        scores(3, 2, (0,))
         quantize_a(4, made[4])
+        scores(3, 3, (1,))
         quantize_a(5, made[5])
-        made[6] = layer_a(6, picked[3], 20)[:]
-        scores(4)
+        for g in range(GROUPS):
+            layer_a(6, g, picked[3], made[6], 4 + g)
+        scores(4, 6)
         quantize_a(6, made[6])
-        scores(5, (0,))
-        made[7] = layer_a(7, picked[3], 22)[:]
+        scores(5, 0, (0,))
+        layer_a(7, 0, picked[3], made[7], 3)
+        layer_a(7, 1, picked[3], made[7], 6)
         quantize_group(7, 0, made[7])
-        scores(5, (1,))
+        scores(5, 1, (1,))
         quantize_group(7, 1, made[7])
-        scores(6)
-        scores(7, (0,))
-        scores(7, (1,), 0, LOOK)
-        scores(7, (1,), LOOK, LOOK)
+        scores(6, 2, (0,))
+        scores(6, 4, (1,))
+        scores(7, 5, (0,))
+        scores(7, 1, (1,), 2)

@@ -57,7 +57,7 @@ def tile_list_biaff_none_prior_kernel(
         ta_s = held("ta_s", [P, T // 4], I32)
         tb_w = held("tb_w", [P, T], I32)
         tb_s = held("tb_s", [P, T // 4], I32)
-        wa_raw = [held("wa_raw0", [P, PASSES, HALF], I32), placed("wa_raw1", [P, PASSES, HALF], I32, 0)]
+        wa_raw = [placed("wa_raw0", [P, PASSES, HALF], I32, 50), placed("wa_raw1", [P, PASSES, HALF], I32, 0)]
         wb_raw0 = [placed("wb_raw0%d" % a, [P, HALF], I32, 42 + 2 * a) for a in range(PASSES)]
         wb_raw1 = placed("wb_raw1", [P, PASSES, HALF], I32, 46)
         wa_sraw = held("wa_sraw", [P, R // 4], I32)
@@ -328,7 +328,7 @@ def tile_list_biaff_none_prior_kernel(
         reorder_words(wa_w[1], wa_raw[1])
 
         hb_s = {}
-        for h, g, at in ((0, 0, 24), (0, 1, 2.5), (1, 0, 3), (1, 1, 3.5)):
+        for h, g, at in ((0, 0, 50), (0, 1, 2.5), (1, 0, 3), (1, 1, 3.5)):
             hb_s[h, g] = placed("hb_s%d%d" % (h, g), [P, HALF], U8, at)
         made = {}
         picked.append([gather_a(1, a, a) for a in range(PASSES)])
@@ -340,9 +340,9 @@ def tile_list_biaff_none_prior_kernel(
         quantize_b(0, 0)
         quantize_b(0, 1)
         quantize_b(1, 0)
-        early = gather_a(2, 0, 34)
         quantize_b(1, 1)
         quantize_a(0, made[0])
+        early = gather_a(2, 0, 38)
         quantize_a(1, made[1])
         picked.append([early, gather_a(2, 1, 10)])
         made[2], made[3] = layer_a_wide(picked[1], 1, 4)
@@ -353,10 +353,10 @@ def tile_list_biaff_none_prior_kernel(
         picked.append([gather_a(3, a, 14 + a) for a in range(PASSES)])
         made[4], made[5] = layer_a_wide(picked[2], 2, 4)
         scores(2, 0)
-        scores(3, 2, (0,))
         quantize_a(4, made[4])
-        scores(3, 3, (1,))
+        scores(3, 2, (0,))
         quantize_a(5, made[5])
+        scores(3, 3, (1,))
         for g in range(GROUPS):
             layer_a(6, g, picked[3], made[6], 4 + g)
         scores(4, 6)

@@ -62,9 +62,8 @@ def tile_list_biaff_none_prior_kernel(
         wb_raw1 = placed("wb_raw1", [P, PASSES, HALF], I32, 46)
         wa_sraw = held("wa_sraw", [P, R // 4], I32)
         wa_s = held("wa_s", [P, R // 4], I32)
-        wb_sraw = held("wb_sraw", [ROWS, R // 4], I32)
         gb_s = held("gb_s", [P, HALF], U8)
-        b_rows = held("b_rows", [ROWS, (R + HALF) // 4], I32)
+        b_rows = held("b_rows", [ROWS, 2 * R // 4], I32)
         b_planes = held("b_planes", [P, PASSES, (R + HALF) // 4], I32)
         b_late = held("b_late", [P, PASSES, HALF // 4], I32)
         wa_w = [held("wa_w%d" % g, [P, PACK, PASSES, P], I32) for g in range(GROUPS)]
@@ -259,12 +258,13 @@ def tile_list_biaff_none_prior_kernel(
 
         nc.gpsimd.memset(tb_s[32:64, :], 0)
         nc.gpsimd.memset(tb_s[64:128, :], 0)
-        for plane in (wa_sraw, b_planes, b_late, ta_s):
+        nc.gpsimd.memset(b_late[:], 0)
+        for plane in (wa_sraw, b_planes, ta_s):
             nc.vector.memset(plane[:], 0)
 
-        nc.sync.dma_start(list_b[:], offs2)
-        load_rows(nc.sync, wb_sraw[:], wb_scales)
         load_rows(nc.sync, tb_s[0:ROWS, :], tab2_scales)
+        nc.sync.dma_start(list_b[:], offs2)
+        load_rows(nc.sync, b_rows[:, R // 4 :], wb_scales)
         nc.sync.dma_start(out=wb_raw0[0][:], in_=words(wb_words[0])[:, 0:HALF])
         nc.sync.dma_start(out=tb_w[:], in_=words(tab2_words[0]))
         nc.sync.dma_start(out=wb_raw0[1][:], in_=words(wb_words[1])[:, 0:HALF])
@@ -281,10 +281,10 @@ def tile_list_biaff_none_prior_kernel(
                 stop=True,
             )
 
-        reorder_scales(b_rows[:, 0 : R // 4], wb_sraw[:])
         gather_b_scales(gb_s, 0, HALF)
-        nc.vector.tensor_copy(out=b_rows[:, R // 4 :], in_=gb_s[0:ROWS, :].bitcast(I32))
-        spread_rows(b_planes, b_rows)
+        reorder_scales(b_rows[:, 0 : R // 4], b_rows[:, R // 4 :])
+        nc.vector.tensor_copy(out=b_rows[:, R // 4 : (R + HALF) // 4], in_=gb_s[0:ROWS, :].bitcast(I32))
+        spread_rows(b_planes, b_rows[:, 0 : (R + HALF) // 4])
         gb_s_late = after("gb_s", "gb_s_late", [P, HALF], U8)
         gather_b_scales(gb_s_late, HALF, HALF)
         load_weight(wb_raw1, wb_words, 1)

@@ -28,7 +28,8 @@ HALF = 512
 SCORE_SCALE = 0.03125
 ROWS = 32
 SPLIT_STORES = 3
-WARM = 7
+WARM = 5
+WARM_LATE = 2
 BANKS = 8
 BANK_BYTES = 2048
 
@@ -57,20 +58,18 @@ def tile_list_biaff_none_prior_kernel(
         ta_s = held("ta_s", [P, T // 4], I32)
         tb_w = held("tb_w", [P, T], I32)
         tb_s = held("tb_s", [P, T // 4], I32)
-        wa_raw = [placed("wa_raw0", [P, PASSES, HALF], I32, 50), placed("wa_raw1", [P, PASSES, HALF], I32, 0)]
-        wb_raw0 = [placed("wb_raw0%d" % a, [P, HALF], I32, 42 + 2 * a) for a in range(PASSES)]
-        wb_raw1 = placed("wb_raw1", [P, PASSES, HALF], I32, 46)
-        wa_sraw = held("wa_sraw", [P, R // 4], I32)
-        wa_s = held("wa_s", [P, R // 4], I32)
-        gb_s = held("gb_s", [P, HALF], U8)
+        wa_raw = [placed("wa_raw0", [P, PASSES, HALF], I32, 26), placed("wa_raw1", [P, PASSES, HALF], I32, 83)]
+        wb_raw0 = [placed("wb_raw0%d" % a, [P, HALF], I32, 43 - 8 * a) for a in range(PASSES)]
+        wb_raw1 = [placed("wb_raw1%d" % a, [P, HALF], I32, 38 - 8 * a) for a in range(PASSES)]
+        wa_rows = held("wa_rows", [ROWS, R // 4], I32)
         b_rows = held("b_rows", [ROWS, 2 * R // 4], I32)
-        b_planes = held("b_planes", [P, PASSES, (R + HALF) // 4], I32)
-        b_late = held("b_late", [P, PASSES, HALF // 4], I32)
-        wa_w = [held("wa_w%d" % g, [P, PACK, PASSES, P], I32) for g in range(GROUPS)]
+        b_planes = held("b_planes", [P, PASSES, (R + LOOK) // 4], I32)
+        b_mid = held("b_mid", [P, PASSES, HALF // 4], I32)
+        wa_w = {}
         wb_w = [held("wb_w%d" % g, [P, PACK, PASSES, P], I32) for g in range(GROUPS)]
         gb_w = {}
         hb16 = {
-            (h, g): placed("hb16_%d%d" % (h, g), [P, HALF, PACK], BF16, 26 + 8 * h + 4 * g)
+            (h, g): placed("hb16_%d%d" % (h, g), [P, HALF, PACK], BF16, 64 + 8 * h + 4 * g)
             for h in range(J // HALF)
             for g in range(GROUPS)
         }
@@ -86,8 +85,8 @@ def tile_list_biaff_none_prior_kernel(
             view = src.rearrange("a p n t -> p a (n t)").bitcast(I32)
             nc.sync.dma_start(out=dst[:], in_=view[:, :, g * HALF : (g + 1) * HALF])
 
-        def reorder_pass(dst, raw):
-            nc.vector.tensor_copy(
+        def reorder_pass(engine, dst, raw):
+            engine.tensor_copy(
                 out=dst.rearrange("p t (b i) -> p t b i", i=RUN),
                 in_=raw.rearrange("p (b t i) -> p t b i", t=PACK, i=RUN),
             )
@@ -95,26 +94,18 @@ def tile_list_biaff_none_prior_kernel(
         def load_rows(queue, dst, src):
             queue.dma_start(out=dst, in_=src.bitcast(I32).rearrange("a q n -> q a n"))
 
-        def load_packed(dst, src):
-            rows = src.bitcast(I32)
-            for q in range(4):
-                nc.sync.dma_start(out=dst[32 * q : 32 * q + 8, :], in_=rows[:, 4 * q : 4 * q + 4, :])
-
-        def after(slot, name, shape, dtype):
-            return keep.tile(shape, dtype, name=name, tag=slot, align_bytes=256)
-
         def spread_rows(planes, rows):
             for q in range(4):
                 nc.sync.dma_start(out=planes[32 * q : 32 * q + 4, :, :], in_=rows[8 * q : 8 * q + 8, :])
 
-        def reorder_words(dst, raw):
-            nc.vector.tensor_copy(
-                out=dst[:].rearrange("p t a (b i) -> p t (a b) i", i=RUN),
-                in_=raw[:].rearrange("p a (b t i) -> p t (a b) i", t=PACK, i=RUN),
+        def reorder_words(engine, dst, raw, places=slice(0, PACK)):
+            engine.tensor_copy(
+                out=dst[:].rearrange("p t a (b i) -> p t (a b) i", i=RUN)[:, places],
+                in_=raw[:].rearrange("p a (b t i) -> p t (a b) i", t=PACK, i=RUN)[:, places],
             )
 
-        def reorder_scales(dst_flat, raw_flat):
-            nc.vector.tensor_copy(
+        def reorder_scales(engine, dst_flat, raw_flat):
+            engine.tensor_copy(
                 out=dst_flat.rearrange("p (t b i) -> p t b i", t=PACK, i=RUN // 4),
                 in_=raw_flat.rearrange("p (b t i) -> p t b i", t=PACK, i=RUN // 4),
             )
@@ -141,6 +132,19 @@ def tile_list_biaff_none_prior_kernel(
             nc.vector.tensor_copy(picked[:], ta_w[a][:].bitcast(U32).indirect(entries(list_a, q)))
             return picked
 
+        def gather_a_scales(h, kib, width):
+            rows = placed("ga_s%d" % h, [P, width], U8, kib)[:, :HALF]
+            nc.vector.tensor_copy(rows, ta_s[:].bitcast(U8).indirect(list_a[:, h * HALF // 16 : (h + 1) * HALF // 16]))
+            spread_rows(ga_planes[h], rows.bitcast(I32))
+
+        def a_scale(a, first, count):
+            inner = first % HALF
+            return ga_planes[first // HALF][:, a, inner // 4 : (inner + count) // 4].bitcast(U8)
+
+        def load_prior(tiles):
+            for i in tiles:
+                nc.sync.dma_start(out=prior[i][:], in_=pr[i * CH : (i + 1) * CH, :])
+
         def weight_scale(planes, a, t, g):
             first = (t * GROUPS + g) * P // 4
             return planes[:, a, first : first + P // 4].bitcast(U8)
@@ -148,24 +152,33 @@ def tile_list_biaff_none_prior_kernel(
         def interleave(dst, bank):
             nc.scalar.copy(out=dst, in_=bank[:].rearrange("p (t n) -> p n t", t=PACK))
 
-        def layer_b(c, g, n):
-            bank = bank_at("bank_b%d%d" % (c, g), n)
-            early = c * CH < HALF
-            planes = b_planes if early else b_late
-            first = (R + c * CH) // 4 if early else (c * CH - HALF) // 4
-            for t in range(PACK):
-                for a in range(PASSES):
-                    nc.tensor.matmul_mx(
-                        out=bank[:, t * CH : (t + 1) * CH],
-                        lhsT=wb_w[g][:, t, a, :].bitcast(FP8X4),
-                        lhsT_scale=weight_scale(b_planes, a, t, g),
-                        rhs=gb_w[c][:, a, :].bitcast(FP4X4),
-                        rhs_scale=planes[:, a, first : first + CH // 4].bitcast(U8),
-                        start=(a == 0),
-                        stop=(a == PASSES - 1),
-                    )
+        def pass_b(bank, c, g, t, a, start, stop):
+            if c * CH < LOOK:
+                planes, first = b_planes, (R + c * CH) // 4
+            elif c * CH < LOOK + HALF:
+                planes, first = b_mid, (c * CH - LOOK) // 4
+            else:
+                planes, first = a_planes, (R + c * CH - LOOK - HALF) // 4
+            nc.tensor.matmul_mx(
+                out=bank[:, t * CH : (t + 1) * CH],
+                lhsT=wb_w[g][:, t, a, :].bitcast(FP8X4),
+                lhsT_scale=weight_scale(b_planes, a, t, g),
+                rhs=gb_w[c][:, a, :].bitcast(FP4X4),
+                rhs_scale=planes[:, a, first : first + CH // 4].bitcast(U8),
+                start=start,
+                stop=stop,
+            )
+
+        def empty_b(bank, c, g):
             inner = c * CH % HALF
             interleave(hb16[c * CH // HALF, g][:, inner : inner + CH, :], bank)
+
+        def layer_b(c, g, n):
+            bank = bank_at("bank_b%d%d" % (c, g), n)
+            for t in range(PACK):
+                for a in range(PASSES):
+                    pass_b(bank, c, g, t, a, a == 0, a == PASSES - 1)
+            empty_b(bank, c, g)
 
         def quantize_b(h, g):
             nc.vector.quantize_mx(
@@ -178,14 +191,13 @@ def tile_list_biaff_none_prior_kernel(
             first = c * CH % LOOK
             bank = bank_at("bank_a%d%d" % (c, g), n)
             for t in range(PACK):
-                word = (t * GROUPS + g) * P // 4
                 for a in range(PASSES):
                     nc.tensor.matmul_mx(
                         out=bank[:, t * CH : (t + 1) * CH],
                         lhsT=wa_w[g][:, t, a, :].bitcast(FP8X4),
-                        lhsT_scale=wa_s[4 * a :, word : word + P // 4].bitcast(U8),
+                        lhsT_scale=weight_scale(a_planes, a, t, g),
                         rhs=picked[a][:, first : first + CH].bitcast(FP8X4),
-                        rhs_scale=ga_all[4 * a :, c * CH : (c + 1) * CH],
+                        rhs_scale=a_scale(a, c * CH, CH),
                         start=(a == 0),
                         stop=(a == PASSES - 1),
                     )
@@ -198,14 +210,13 @@ def tile_list_biaff_none_prior_kernel(
                     bank = bank_at("bank_w%d%d%d" % (q, g, u), n + 2 * g + u)
                     for e in range(2):
                         t = 2 * u + e
-                        word = (t * GROUPS + g) * P // 4
                         for a in range(PASSES):
                             nc.tensor.matmul_mx(
                                 out=bank[:, e * LOOK : (e + 1) * LOOK],
                                 lhsT=wa_w[g][:, t, a, :].bitcast(FP8X4),
-                                lhsT_scale=wa_s[4 * a :, word : word + P // 4].bitcast(U8),
+                                lhsT_scale=weight_scale(a_planes, a, t, g),
                                 rhs=picked[a][:].bitcast(FP8X4),
-                                rhs_scale=ga_all[4 * a :, q * LOOK : (q + 1) * LOOK],
+                                rhs_scale=a_scale(a, q * LOOK, LOOK),
                                 start=(a == 0),
                                 stop=(a == PASSES - 1),
                             )
@@ -258,8 +269,7 @@ def tile_list_biaff_none_prior_kernel(
 
         nc.gpsimd.memset(tb_s[32:64, :], 0)
         nc.gpsimd.memset(tb_s[64:128, :], 0)
-        nc.gpsimd.memset(b_late[:], 0)
-        for plane in (wa_sraw, b_planes, ta_s):
+        for plane in (ta_s, b_planes, b_mid):
             nc.vector.memset(plane[:], 0)
 
         load_rows(nc.sync, tb_s[0:ROWS, :], tab2_scales)
@@ -270,68 +280,94 @@ def tile_list_biaff_none_prior_kernel(
         nc.sync.dma_start(out=wb_raw0[1][:], in_=words(wb_words[1])[:, 0:HALF])
 
         warm = bank_at("warm", BANKS - 1)
-        for i in range(WARM):
+        for i in range(WARM + WARM_LATE):
             nc.tensor.matmul_mx(
                 out=warm[:],
-                lhsT=wb_raw0[0][:, 0:P].bitcast(FP8X4),
-                lhsT_scale=wa_sraw[:].bitcast(U8)[:, 0:P],
+                lhsT=wb_raw0[0 if i < WARM else 1][:, 0:P].bitcast(FP8X4),
+                lhsT_scale=ta_s[:, 0 : P // 4].bitcast(U8),
                 rhs=wb_raw0[0][:].bitcast(FP8X4),
-                rhs_scale=wa_sraw[:].bitcast(U8)[:, 0:HALF],
+                rhs_scale=ta_s[:, 0 : HALF // 4].bitcast(U8),
                 start=True,
                 stop=True,
             )
 
-        gather_b_scales(gb_s, 0, HALF)
-        reorder_scales(b_rows[:, 0 : R // 4], b_rows[:, R // 4 :])
-        nc.vector.tensor_copy(out=b_rows[:, R // 4 : (R + HALF) // 4], in_=gb_s[0:ROWS, :].bitcast(I32))
-        spread_rows(b_planes, b_rows[:, 0 : (R + HALF) // 4])
-        gb_s_late = after("gb_s", "gb_s_late", [P, HALF], U8)
-        gather_b_scales(gb_s_late, HALF, HALF)
-        load_weight(wb_raw1, wb_words, 1)
-        nc.sync.dma_start(list_a[:], offs)
-        load_packed(ta_s, tab_scales)
-        nc.sync.dma_start(out=ta_w[0][:], in_=words(tab_words[0]))
-
-        pairs = held("pairs0", [P, LOOK], U32)
-        gather_b_words(0, pairs[:])
+        gb_s0 = placed("gb_s0", [P, HALF], U8, 57)[:, :LOOK]
+        gather_b_scales(gb_s0, 0, LOOK)
+        reorder_scales(nc.vector, b_rows[:, 0 : R // 4], b_rows[:, R // 4 :])
+        nc.vector.tensor_copy(out=b_rows[:, R // 4 : (R + LOOK) // 4], in_=gb_s0[0:ROWS, :].bitcast(I32))
+        spread_rows(b_planes, b_rows[:, 0 : (R + LOOK) // 4])
+        reorder_pass(nc.vector, wb_w[0][:, :, 0, :], wb_raw0[0][:])
+        gb_s1 = placed("gb_s1", [P, HALF], U8, 56.75)
+        gather_b_scales(gb_s1, LOOK, HALF)
+        a_planes = placed("a_planes", [P, PASSES, (R + LOOK) // 4], I32, 57.25)
+        nc.gpsimd.memset(a_planes[:], 0)
         for a in range(PASSES):
-            reorder_pass(wb_w[0][:, :, a, :], wb_raw0[a][:])
-        part(placed("gb_w0", [P, PASSES, 2 * CH], U8, 44), pairs[:, :CH], 0)
-        part(placed("gb_w1", [P, PASSES, 2 * CH], U8, 44.5), pairs[:, CH:], 1)
-        pairs = placed("pairs1", [P, LOOK], U32, 45)
-        gather_b_words(1, pairs[:])
-        part(held("gb_w2", [P, PASSES, 2 * CH], U8), pairs[:, :CH], 2)
-        part(held("gb_w3", [P, PASSES, 2 * CH], U8), pairs[:, CH:], 3)
-        reorder_words(wb_w[1], wb_raw1)
-        spread_rows(b_late, gb_s_late[:].bitcast(I32))
-        nc.sync.dma_start(out=ta_w[1][:], in_=words(tab_words[1]))
-        load_packed(wa_sraw, wa_scales)
+            nc.sync.dma_start(out=wb_raw1[a][:], in_=words(wb_words[a])[:, HALF:])
         load_weight(wa_raw[0], wa_words, 0)
+        load_rows(nc.sync, wa_rows[:], wa_scales)
+        spread_rows(b_mid, gb_s1[:].bitcast(I32))
+        nc.sync.dma_start(out=ta_w[0][:], in_=words(tab_words[0]))
+        load_rows(nc.sync, ta_s[0:ROWS, :], tab_scales)
+        nc.sync.dma_start(list_a[:], offs)
+        nc.sync.dma_start(out=ta_w[1][:, : T // 2], in_=words(tab_words[1])[:, : T // 2])
+
+        pairs = placed("pairs0", [P, LOOK], U32, 54)
+        gather_b_words(0, pairs[:])
+        part(held("gb_w0", [P, PASSES, 2 * CH], U8), pairs[:, :CH], 0)
+        part(held("gb_w1", [P, PASSES, 2 * CH], U8), pairs[:, CH:], 1)
+        reorder_pass(nc.vector, wb_w[0][:, :, 1, :], wb_raw0[1][:])
+        reorder_pass(nc.gpsimd, wb_w[1][:, :, 0, :], wb_raw1[0][:])
+        pairs = placed("pairs1", [P, LOOK], U32, 53.5)
+        gather_b_words(1, pairs[:])
+        reorder_pass(nc.vector, wb_w[1][:, :, 1, :], wb_raw1[1][:])
+        part(placed("gb_w2", [P, PASSES, 2 * LOOK], U8, 38), pairs[:], 2)
+        a_rows = placed("a_rows", [ROWS, (R + LOOK) // 4], I32, 52.5)
+        reorder_scales(nc.gpsimd, a_rows[:, 0 : R // 4], wa_rows[:])
+        wa_w[0] = held("wa_w0", [P, PACK, PASSES, P], I32)
+        reorder_words(nc.gpsimd, wa_w[0], wa_raw[0])
+        gb_s2 = placed("gb_s2", [P, LOOK], U8, 30)
+        gather_b_scales(gb_s2, LOOK + HALF, LOOK)
+        pairs = placed("pairs2", [P, LOOK], U32, 30.25)
+        gather_b_words(2, pairs[:])
+        last_pairs = placed("pairs3", [P, LOOK], U32, 31.25)
+        gather_b_words(3, last_pairs[:])
+        nc.vector.tensor_copy(out=a_rows[:, R // 4 :], in_=gb_s2[0:ROWS, :].bitcast(I32))
+        part(held("gb_w4", [P, PASSES, 2 * LOOK], U8), pairs[:], 4)
+        part(held("gb_w6", [P, PASSES, 2 * LOOK], U8), last_pairs[:], 6)
+        spread_rows(a_planes, a_rows)
+        nc.sync.dma_start(out=ta_w[1][:, T // 2 :], in_=words(tab_words[1])[:, T // 2 :])
         load_weight(wa_raw[1], wa_words, 1)
-        for i in range(M // CH):
-            nc.sync.dma_start(out=prior[i][:], in_=pr[i * CH : (i + 1) * CH, :])
+        ga_planes = [placed("ga_planes%d" % h, [P, PASSES, HALF // 4], I32, 30.75 + h) for h in range(2)]
+        for h in range(2):
+            nc.gpsimd.memset(ga_planes[h][:], 0)
+        gather_a_scales(0, 80, 3 * M)
+        wa_w[1] = held("wa_w1", [P, PACK, PASSES, P], I32)
+        reorder_words(nc.gpsimd, wa_w[1], wa_raw[1])
 
-        for q in (2, 3):
-            pairs = placed("pairs%d" % q, [P, LOOK], U32, 45 + q)
-            gather_b_words(q, pairs[:])
-            part(held("gb_w%d" % (2 * q), [P, PASSES, 2 * LOOK], U8), pairs[:], 2 * q)
-        for h in range(J // HALF):
+        for g in range(GROUPS):
+            banks = [bank_at("bank_b%d%d" % (c, g), 2 * g + c) for c in range(2)]
+            for a in range(PASSES):
+                for c in range(2):
+                    for t in range(PACK):
+                        pass_b(banks[c], c, g, t, a, a == 0 and t == 0, a == PASSES - 1 and t == PACK - 1)
+            for c in range(2):
+                empty_b(banks[c], c, g)
+        for q in range(1, J // LOOK):
             for g in range(GROUPS):
-                for c in range(h * HALF // CH, (h + 1) * HALF // CH):
-                    layer_b(c, g, (g * HALF // CH + c) % BANKS if h == 0 else (g * HALF // CH + c - HALF // CH) % BANKS)
+                for c in (2 * q, 2 * q + 1):
+                    layer_b(c, g, (4 * q + 2 * g + c % 2) % BANKS)
 
-        ga_all = held("ga_all", [P, M], U8)
-        nc.vector.tensor_copy(ga_all[:], ta_s[:].bitcast(U8).indirect(list_a[:]))
-        picked = [[gather_a(0, a, 4 + a) for a in range(PASSES)]]
-        reorder_scales(wa_s[:], wa_sraw[:])
-        reorder_words(wa_w[0], wa_raw[0])
-        reorder_words(wa_w[1], wa_raw[1])
+        picked = [[gather_a(q, 0, 4 + 2 * q)] for q in range(2)]
+        for q in range(2):
+            picked[q].append(gather_a(q, 1, 5 + 2 * q))
+        load_prior(range(0, 3))
+        gather_a_scales(1, 80, HALF)
+        load_prior(range(3, M // CH))
 
         hb_s = {}
-        for h, g, at in ((0, 0, 50), (0, 1, 2.5), (1, 0, 3), (1, 1, 3.5)):
+        for h, g, at in ((0, 0, 82.75), (0, 1, 80.5), (1, 0, 81), (1, 1, 81.5)):
             hb_s[h, g] = placed("hb_s%d%d" % (h, g), [P, HALF], U8, at)
         made = {}
-        picked.append([gather_a(1, a, a) for a in range(PASSES)])
         for c, kib in ((0, 8), (1, 10), (6, 20), (7, 22)):
             made[c] = placed("ha16_%d" % c, [P, GROUPS, CH, PACK], BF16, kib)[:]
         for g in range(GROUPS):
@@ -342,9 +378,8 @@ def tile_list_biaff_none_prior_kernel(
         quantize_b(1, 0)
         quantize_b(1, 1)
         quantize_a(0, made[0])
-        early = gather_a(2, 0, 38)
         quantize_a(1, made[1])
-        picked.append([early, gather_a(2, 1, 10)])
+        picked.append([gather_a(2, a, 8 + a) for a in range(PASSES)])
         made[2], made[3] = layer_a_wide(picked[1], 1, 4)
         scores(0, 0)
         scores(1, 2)

@@ -95,7 +95,7 @@ def tile_list_biaff_none_prior_kernel(
             queue.dma_start(out=dst, in_=src.bitcast(I32).rearrange("a q n -> q a n"))
 
         def spread_rows(planes, rows):
-            for q in range(4):
+            for q in (0, 2, 1, 3):
                 nc.sync.dma_start(out=planes[32 * q : 32 * q + 4, :, :], in_=rows[8 * q : 8 * q + 8, :])
 
         def reorder_words(engine, dst, raw, places=slice(0, PACK)):

@@ -173,12 +173,14 @@ def tile_list_biaff_none_prior_kernel(
             inner = c * CH % HALF
             interleave(hb16[c * CH // HALF, g][:, inner : inner + CH, :], bank)
 
-        def layer_b(c, g, n):
-            bank = bank_at("bank_b%d%d" % (c, g), n)
+        def layer_b(q, g, n):
+            banks = [bank_at("bank_b%d%d" % (2 * q + e, g), n + e) for e in range(2)]
             for t in range(PACK):
                 for a in range(PASSES):
-                    pass_b(bank, c, g, t, a, a == 0, a == PASSES - 1)
-            empty_b(bank, c, g)
+                    for e in range(2):
+                        pass_b(banks[e], 2 * q + e, g, t, a, a == 0, a == PASSES - 1)
+            for e in range(2):
+                empty_b(banks[e], 2 * q + e, g)
 
         def quantize_b(h, g):
             nc.vector.quantize_mx(
@@ -202,6 +204,23 @@ def tile_list_biaff_none_prior_kernel(
                         stop=(a == PASSES - 1),
                     )
             interleave(ha16[:, g, :, :], bank)
+
+        def layer_a_pair(g, picked, made, n):
+            banks = [bank_at("bank_a%d%d" % (c, g), n + c) for c in range(2)]
+            for t in range(PACK):
+                for a in range(PASSES):
+                    for c in range(2):
+                        nc.tensor.matmul_mx(
+                            out=banks[c][:, t * CH : (t + 1) * CH],
+                            lhsT=wa_w[g][:, t, a, :].bitcast(FP8X4),
+                            lhsT_scale=weight_scale(a_planes, a, t, g),
+                            rhs=picked[a][:, c * CH : (c + 1) * CH].bitcast(FP8X4),
+                            rhs_scale=a_scale(a, c * CH, CH),
+                            start=(a == 0),
+                            stop=(a == PASSES - 1),
+                        )
+            for c in range(2):
+                interleave(made[c][:, g, :, :], banks[c])
 
         def layer_a_wide(picked, q, n):
             both = placed("both16_%d" % q, [P, 2, GROUPS, CH, PACK], BF16, 8 + 4 * q)
@@ -347,15 +366,14 @@ def tile_list_biaff_none_prior_kernel(
         for g in range(GROUPS):
             banks = [bank_at("bank_b%d%d" % (c, g), 2 * g + c) for c in range(2)]
             for a in range(PASSES):
-                for c in range(2):
-                    for t in range(PACK):
-                        pass_b(banks[c], c, g, t, a, a == 0 and t == 0, a == PASSES - 1 and t == PACK - 1)
+                order = [(c, t) for t in range(PACK) for c in range(2)]
+                for c, t in sorted(order) if g == 0 and a == 0 else order:
+                    pass_b(banks[c], c, g, t, a, a == 0 and t == 0, a == PASSES - 1 and t == PACK - 1)
             for c in range(2):
                 empty_b(banks[c], c, g)
         for q in range(1, J // LOOK):
             for g in range(GROUPS):
-                for c in (2 * q, 2 * q + 1):
-                    layer_b(c, g, (4 * q + 2 * g + c % 2) % BANKS)
+                layer_b(q, g, (4 * q + 2 * g) % BANKS)
 
         picked = [[gather_a(q, 0, 4 + 2 * q)] for q in range(2)]
         for q in range(2):
@@ -371,8 +389,7 @@ def tile_list_biaff_none_prior_kernel(
         for c, kib in ((0, 8), (1, 10), (6, 20), (7, 22)):
             made[c] = placed("ha16_%d" % c, [P, GROUPS, CH, PACK], BF16, kib)[:]
         for g in range(GROUPS):
-            for c in range(2):
-                layer_a(c, g, picked[0], made[c], 2 * g + c)
+            layer_a_pair(g, picked[0], made, 2 * g)
         quantize_b(0, 0)
         quantize_b(0, 1)
         quantize_b(1, 0)

from contextlib import ExitStack

import concourse.mybir as mybir

K, R, T, M, J = 1024, 1024, 2048, 1024, 1024
FLOPS = 2 * K * R * M + 2 * K * R * J + 2 * R * M * J

F32 = mybir.dt.float32
BF16 = mybir.dt.bfloat16
I32 = mybir.dt.int32
U32 = mybir.dt.uint32
U16 = mybir.dt.uint16
U8 = mybir.dt.uint8
FP8X4 = mybir.dt.float8_e4m3fn_x4
FP4X4 = mybir.dt.float4_e2m1fn_x4
MULT = mybir.AluOpType.mult
ADD = mybir.AluOpType.add

P = 128
PACK = 4
PASSES = 2
GROUPS = 2
RUN = 8
BLOCKS = 16
CH = 128
LOOK = 256
HALF = 512
SCORE_SCALE = 0.03125
ROWS = 32
SPLIT_STORES = 3
WARM = 5
WARM_LATE = 2
BANKS = 8
BANK_BYTES = 2048


def tile_list_biaff_none_prior_kernel(
    tc, tab_words, tab_scales, tab2_words, tab2_scales, wa_words, wa_scales, wb_words, wb_scales, pr, offs, offs2, out
):
    nc = tc.nc
    with ExitStack() as ctx:
        keep = ctx.enter_context(tc.tile_pool(name="keep", bufs=1))
        tied = ctx.enter_context(tc.tile_pool(name="tied", bufs=1))
        psum = ctx.enter_context(tc.psum_pool(name="psum", bufs=1))

        def held(name, shape, dtype):
            return keep.tile(shape, dtype, name=name, align_bytes=256)

        def placed(name, shape, dtype, kib):
            return tied.tile(shape, dtype, name=name, align_bytes=256, offset=int(kib * 1024))

        def bank_at(name, n):
            return psum.tile([P, HALF], F32, name=name, offset=n * BANK_BYTES)

        list_a = keep.tile([P, M // 16], U16, name="list_a")
        list_b = keep.tile([P, J // 16], U16, name="list_b")
        ta_w = [held("ta_w%d" % a, [P, T], I32) for a in range(PASSES)]
        ta_s = held("ta_s", [P, T // 4], I32)
        tb_w = held("tb_w", [P, T], I32)
        tb_s = held("tb_s", [P, T // 4], I32)
        wa_raw = [placed("wa_raw0", [P, PASSES, HALF], I32, 26), placed("wa_raw1", [P, PASSES, HALF], I32, 83)]
        wb_raw0 = [placed("wb_raw0%d" % a, [P, HALF], I32, 43 - 8 * a) for a in range(PASSES)]
        wb_raw1 = [placed("wb_raw1%d" % a, [P, HALF], I32, 38 - 8 * a) for a in range(PASSES)]
        wa_rows = held("wa_rows", [ROWS, R // 4], I32)
        b_rows = held("b_rows", [ROWS, 2 * R // 4], I32)
        b_planes = held("b_planes", [P, PASSES, (R + LOOK) // 4], I32)
        b_mid = held("b_mid", [P, PASSES, HALF // 4], I32)
        wa_w = {}
        wb_w = [held("wb_w%d" % g, [P, PACK, PASSES, P], I32) for g in range(GROUPS)]
        gb_w = {}
        hb16 = {
            (h, g): placed("hb16_%d%d" % (h, g), [P, HALF, PACK], BF16, 64 + 8 * h + 4 * g)
            for h in range(J // HALF)
            for g in range(GROUPS)
        }
        hb_w = [held("hb_w%d" % h, [P, GROUPS, HALF], U32) for h in range(J // HALF)]
        ha_w = held("ha_w", [P, M // CH, GROUPS, CH], U32)
        ha_s = held("ha_s", [P, M // CH, GROUPS, CH], U8)
        prior = [held("prior%d" % i, [P, J], F32) for i in range(M // CH)]

        def words(src):
            return src.rearrange("p n t -> p (n t)").bitcast(I32)

        def load_weight(dst, src, g):
            view = src.rearrange("a p n t -> p a (n t)").bitcast(I32)
            nc.sync.dma_start(out=dst[:], in_=view[:, :, g * HALF : (g + 1) * HALF])

        def reorder_pass(engine, dst, raw):
            engine.tensor_copy(
                out=dst.rearrange("p t (b i) -> p t b i", i=RUN),
                in_=raw.rearrange("p (b t i) -> p t b i", t=PACK, i=RUN),
            )

        def load_rows(queue, dst, src):
            queue.dma_start(out=dst, in_=src.bitcast(I32).rearrange("a q n -> q a n"))

        def spread_rows(planes, rows):
            for q in (0, 2, 1, 3):
                nc.sync.dma_start(out=planes[32 * q : 32 * q + 4, :, :], in_=rows[8 * q : 8 * q + 8, :])

        def reorder_words(engine, dst, raw, places=slice(0, PACK)):
            engine.tensor_copy(
                out=dst[:].rearrange("p t a (b i) -> p t (a b) i", i=RUN)[:, places],
                in_=raw[:].rearrange("p a (b t i) -> p t (a b) i", t=PACK, i=RUN)[:, places],
            )

        def reorder_scales(engine, dst_flat, raw_flat):
            engine.tensor_copy(
                out=dst_flat.rearrange("p (t b i) -> p t b i", t=PACK, i=RUN // 4),
                in_=raw_flat.rearrange("p (b t i) -> p t b i", t=PACK, i=RUN // 4),
            )

        def entries(lst, q):
            return lst[:, q * LOOK // 16 : (q + 1) * LOOK // 16]

        def gather_b_scales(dst, first, count):
            nc.vector.tensor_copy(dst[:], tb_s[:].bitcast(U8).indirect(list_b[:, first // 16 : (first + count) // 16]))

        def gather_b_words(q, pairs):
            nc.vector.tensor_copy(pairs, tb_w[:].bitcast(U32).indirect(entries(list_b, q)))

        def part(dst, pairs, c):
            nc.vector.tensor_copy(
                out=dst[:].bitcast(U16),
                in_=pairs.bitcast(U16).rearrange("p (n d) -> p d n", d=PASSES),
            )
            for i in range(dst.shape[2] // (2 * CH)):
                gb_w[c + i] = dst[:, :, 2 * i * CH : 2 * (i + 1) * CH]

        def gather_a(q, a, kib):
            picked = placed("ga_w%d%d" % (q, a), [P, LOOK], U32, kib)
            nc.vector.tensor_copy(picked[:], ta_w[a][:].bitcast(U32).indirect(entries(list_a, q)))
            return picked

        def gather_a_scales(h, kib, width):
            rows = placed("ga_s%d" % h, [P, width], U8, kib)[:, :HALF]
            nc.vector.tensor_copy(rows, ta_s[:].bitcast(U8).indirect(list_a[:, h * HALF // 16 : (h + 1) * HALF // 16]))
            spread_rows(ga_planes[h], rows.bitcast(I32))

        def a_scale(a, first, count):
            inner = first % HALF
            return ga_planes[first // HALF][:, a, inner // 4 : (inner + count) // 4].bitcast(U8)

        def load_prior(tiles):
            for i in tiles:
                nc.sync.dma_start(out=prior[i][:], in_=pr[i * CH : (i + 1) * CH, :])

        def weight_scale(planes, a, t, g):
            first = (t * GROUPS + g) * P // 4
            return planes[:, a, first : first + P // 4].bitcast(U8)

        def interleave(dst, bank):
            nc.scalar.copy(out=dst, in_=bank[:].rearrange("p (t n) -> p n t", t=PACK))

        def pass_b(bank, c, g, t, a, start, stop):
            if c * CH < LOOK:
                planes, first = b_planes, (R + c * CH) // 4
            elif c * CH < LOOK + HALF:
                planes, first = b_mid, (c * CH - LOOK) // 4
            else:
                planes, first = a_planes, (R + c * CH - LOOK - HALF) // 4
            nc.tensor.matmul_mx(
                out=bank[:, t * CH : (t + 1) * CH],
                lhsT=wb_w[g][:, t, a, :].bitcast(FP8X4),
                lhsT_scale=weight_scale(b_planes, a, t, g),
                rhs=gb_w[c][:, a, :].bitcast(FP4X4),
                rhs_scale=planes[:, a, first : first + CH // 4].bitcast(U8),
                start=start,
                stop=stop,
            )

        def empty_b(bank, c, g):
            inner = c * CH % HALF
            interleave(hb16[c * CH // HALF, g][:, inner : inner + CH, :], bank)

        def layer_b(q, g, n):
            banks = [bank_at("bank_b%d%d" % (2 * q + e, g), n + e) for e in range(2)]
            for t in range(PACK):
                for a in range(PASSES):
                    for e in range(2):
                        pass_b(banks[e], 2 * q + e, g, t, a, a == 0, a == PASSES - 1)
            for e in range(2):
                empty_b(banks[e], 2 * q + e, g)

        def quantize_b(h, g):
            nc.vector.quantize_mx(
                out=hb_w[h][:, g, :].bitcast(FP8X4),
                scales=hb_s[h, g][:],
                in_=hb16[h, g][:].rearrange("p n t -> p (n t)"),
            )

        def layer_a(c, g, picked, ha16, n):
            first = c * CH % LOOK
            bank = bank_at("bank_a%d%d" % (c, g), n)
            for t in range(PACK):
                for a in range(PASSES):
                    nc.tensor.matmul_mx(
                        out=bank[:, t * CH : (t + 1) * CH],
                        lhsT=wa_w[g][:, t, a, :].bitcast(FP8X4),
                        lhsT_scale=weight_scale(a_planes, a, t, g),
                        rhs=picked[a][:, first : first + CH].bitcast(FP8X4),
                        rhs_scale=a_scale(a, c * CH, CH),
                        start=(a == 0),
                        stop=(a == PASSES - 1),
                    )
            interleave(ha16[:, g, :, :], bank)

        def layer_a_pair(g, picked, made, n):
            banks = [bank_at("bank_a%d%d" % (c, g), n + c) for c in range(2)]
            for t in range(PACK):
                for a in range(PASSES):
                    for c in range(2):
                        nc.tensor.matmul_mx(
                            out=banks[c][:, t * CH : (t + 1) * CH],
                            lhsT=wa_w[g][:, t, a, :].bitcast(FP8X4),
                            lhsT_scale=weight_scale(a_planes, a, t, g),
                            rhs=picked[a][:, c * CH : (c + 1) * CH].bitcast(FP8X4),
                            rhs_scale=a_scale(a, c * CH, CH),
                            start=(a == 0),
                            stop=(a == PASSES - 1),
                        )
            for c in range(2):
                interleave(made[c][:, g, :, :], banks[c])

        def layer_a_wide(picked, q, n):
            both = placed("both16_%d" % q, [P, 2, GROUPS, CH, PACK], BF16, 8 + 4 * q)
            for g in range(GROUPS):
                for u in range(2):
                    bank = bank_at("bank_w%d%d%d" % (q, g, u), n + 2 * g + u)
                    for e in range(2):
                        t = 2 * u + e
                        for a in range(PASSES):
                            nc.tensor.matmul_mx(
                                out=bank[:, e * LOOK : (e + 1) * LOOK],
                                lhsT=wa_w[g][:, t, a, :].bitcast(FP8X4),
                                lhsT_scale=weight_scale(a_planes, a, t, g),
                                rhs=picked[a][:].bitcast(FP8X4),
                                rhs_scale=a_scale(a, q * LOOK, LOOK),
                                start=(a == 0),
                                stop=(a == PASSES - 1),
                            )
                    src = bank[:].rearrange("p (e c n) -> p c n e", e=2, c=2)
                    nc.scalar.copy(out=both[:, :, g, :, 2 * u : 2 * u + 2], in_=src)
            return both[:, 0], both[:, 1]

        def quantize_a(c, ha16):
            nc.vector.quantize_mx(
                out=ha_w[:, c, :, :].rearrange("p g n -> p (g n)").bitcast(FP8X4),
                scales=ha_s[:, c, :, :].rearrange("p g n -> p (g n)"),
                in_=ha16.rearrange("p g n t -> p (g n t)"),
            )

        def quantize_group(c, g, ha16):
            nc.vector.quantize_mx(
                out=ha_w[:, c, g, :].bitcast(FP8X4),
                scales=ha_s[:, c, g, :],
                in_=ha16[:, g, :, :].rearrange("p n t -> p (n t)"),
            )

        def scores(c, n, halves=(0, 1), pieces=1):
            for h in halves:
                bank = bank_at("bank_s%d%d%d" % (c, h, 0), n + h - halves[0])
                for g in range(GROUPS):
                    nc.tensor.matmul_mx(
                        out=bank[:],
                        lhsT=ha_w[:, c, g, :].bitcast(FP8X4),
                        lhsT_scale=ha_s[:, c, g, :],
                        rhs=hb_w[h][:, g, :].bitcast(FP8X4),
                        rhs_scale=hb_s[h, g][:],
                        start=(g == 0),
                        stop=(g == GROUPS - 1),
                    )
                width = HALF // pieces
                for first in range(0, HALF, width):
                    cols = slice(h * HALF + first, h * HALF + first + width)
                    nc.vector.scalar_tensor_tensor(
                        out=prior[c][:, cols],
                        in0=bank[:, first : first + width],
                        scalar=SCORE_SCALE,
                        in1=prior[c][:, cols],
                        op0=MULT,
                        op1=ADD,
                    )
                    if c >= M // CH - SPLIT_STORES:
                        nc.sync.dma_start(out=out[c * CH : (c + 1) * CH, cols], in_=prior[c][:, cols])
            if c < M // CH - SPLIT_STORES and 1 in halves:
                nc.sync.dma_start(out=out[c * CH : (c + 1) * CH, :], in_=prior[c][:])

        nc.gpsimd.memset(tb_s[32:64, :], 0)
        nc.gpsimd.memset(tb_s[64:128, :], 0)
        for plane in (ta_s, b_planes, b_mid):
            nc.vector.memset(plane[:], 0)

        load_rows(nc.sync, tb_s[0:ROWS, :], tab2_scales)
        nc.sync.dma_start(list_b[:], offs2)
        load_rows(nc.sync, b_rows[:, R // 4 :], wb_scales)
        nc.sync.dma_start(out=wb_raw0[0][:], in_=words(wb_words[0])[:, 0:HALF])
        nc.sync.dma_start(out=tb_w[:], in_=words(tab2_words[0]))
        nc.sync.dma_start(out=wb_raw0[1][:], in_=words(wb_words[1])[:, 0:HALF])

        warm = bank_at("warm", BANKS - 1)
        for i in range(WARM + WARM_LATE):
            nc.tensor.matmul_mx(
                out=warm[:],
                lhsT=wb_raw0[0 if i < WARM else 1][:, 0:P].bitcast(FP8X4),
                lhsT_scale=ta_s[:, 0 : P // 4].bitcast(U8),
                rhs=wb_raw0[0][:].bitcast(FP8X4),
                rhs_scale=ta_s[:, 0 : HALF // 4].bitcast(U8),
                start=True,
                stop=True,
            )

        gb_s0 = placed("gb_s0", [P, HALF], U8, 57)[:, :LOOK]
        gather_b_scales(gb_s0, 0, LOOK)
        reorder_scales(nc.vector, b_rows[:, 0 : R // 4], b_rows[:, R // 4 :])
        nc.vector.tensor_copy(out=b_rows[:, R // 4 : (R + LOOK) // 4], in_=gb_s0[0:ROWS, :].bitcast(I32))
        spread_rows(b_planes, b_rows[:, 0 : (R + LOOK) // 4])
        reorder_pass(nc.vector, wb_w[0][:, :, 0, :], wb_raw0[0][:])
        gb_s1 = placed("gb_s1", [P, HALF], U8, 56.75)
        gather_b_scales(gb_s1, LOOK, HALF)
        a_planes = placed("a_planes", [P, PASSES, (R + LOOK) // 4], I32, 57.25)
        nc.gpsimd.memset(a_planes[:], 0)
        for a in range(PASSES):
            nc.sync.dma_start(out=wb_raw1[a][:], in_=words(wb_words[a])[:, HALF:])
        load_weight(wa_raw[0], wa_words, 0)
        load_rows(nc.sync, wa_rows[:], wa_scales)
        spread_rows(b_mid, gb_s1[:].bitcast(I32))
        nc.sync.dma_start(out=ta_w[0][:], in_=words(tab_words[0]))
        load_rows(nc.sync, ta_s[0:ROWS, :], tab_scales)
        nc.sync.dma_start(list_a[:], offs)
        nc.sync.dma_start(out=ta_w[1][:, : T // 2], in_=words(tab_words[1])[:, : T // 2])

        pairs = placed("pairs0", [P, LOOK], U32, 54)
        gather_b_words(0, pairs[:])
        part(held("gb_w0", [P, PASSES, 2 * CH], U8), pairs[:, :CH], 0)
        part(held("gb_w1", [P, PASSES, 2 * CH], U8), pairs[:, CH:], 1)
        reorder_pass(nc.vector, wb_w[0][:, :, 1, :], wb_raw0[1][:])
        reorder_pass(nc.gpsimd, wb_w[1][:, :, 0, :], wb_raw1[0][:])
        pairs = placed("pairs1", [P, LOOK], U32, 53.5)
        gather_b_words(1, pairs[:])
        reorder_pass(nc.vector, wb_w[1][:, :, 1, :], wb_raw1[1][:])
        part(placed("gb_w2", [P, PASSES, 2 * LOOK], U8, 38), pairs[:], 2)
        a_rows = placed("a_rows", [ROWS, (R + LOOK) // 4], I32, 52.5)
        reorder_scales(nc.gpsimd, a_rows[:, 0 : R // 4], wa_rows[:])
        wa_w[0] = held("wa_w0", [P, PACK, PASSES, P], I32)
        reorder_words(nc.gpsimd, wa_w[0], wa_raw[0])
        gb_s2 = placed("gb_s2", [P, LOOK], U8, 30)
        gather_b_scales(gb_s2, LOOK + HALF, LOOK)
        pairs = placed("pairs2", [P, LOOK], U32, 30.25)
        gather_b_words(2, pairs[:])
        last_pairs = placed("pairs3", [P, LOOK], U32, 31.25)
        gather_b_words(3, last_pairs[:])
        nc.vector.tensor_copy(out=a_rows[:, R // 4 :], in_=gb_s2[0:ROWS, :].bitcast(I32))
        part(held("gb_w4", [P, PASSES, 2 * LOOK], U8), pairs[:], 4)
        part(held("gb_w6", [P, PASSES, 2 * LOOK], U8), last_pairs[:], 6)
        spread_rows(a_planes, a_rows)
        nc.sync.dma_start(out=ta_w[1][:, T // 2 :], in_=words(tab_words[1])[:, T // 2 :])
        load_weight(wa_raw[1], wa_words, 1)
        ga_planes = [placed("ga_planes%d" % h, [P, PASSES, HALF // 4], I32, 30.75 + h) for h in range(2)]
        for h in range(2):
            nc.gpsimd.memset(ga_planes[h][:], 0)
        gather_a_scales(0, 80, 3 * M)
        wa_w[1] = held("wa_w1", [P, PACK, PASSES, P], I32)
        reorder_words(nc.gpsimd, wa_w[1], wa_raw[1])

        for g in range(GROUPS):
            banks = [bank_at("bank_b%d%d" % (c, g), 2 * g + c) for c in range(2)]
            for a in range(PASSES):
                order = [(c, t) for t in range(PACK) for c in range(2)]
                for c, t in sorted(order) if g == 0 and a == 0 else order:
                    pass_b(banks[c], c, g, t, a, a == 0 and t == 0, a == PASSES - 1 and t == PACK - 1)
            for c in range(2):
                empty_b(banks[c], c, g)
        for q in range(1, J // LOOK):
            for g in range(GROUPS):
                layer_b(q, g, (4 * q + 2 * g) % BANKS)

        picked = [[gather_a(q, 0, 4 + 2 * q)] for q in range(2)]
        for q in range(2):
            picked[q].append(gather_a(q, 1, 5 + 2 * q))
        load_prior(range(0, 3))
        gather_a_scales(1, 80, HALF)
        load_prior(range(3, M // CH))

        hb_s = {}
        for h, g, at in ((0, 0, 82.75), (0, 1, 80.5), (1, 0, 81), (1, 1, 81.5)):
            hb_s[h, g] = placed("hb_s%d%d" % (h, g), [P, HALF], U8, at)
        made = {}
        for c, kib in ((0, 8), (1, 10), (6, 20), (7, 22)):
            made[c] = placed("ha16_%d" % c, [P, GROUPS, CH, PACK], BF16, kib)[:]
        for g in range(GROUPS):
            layer_a_pair(g, picked[0], made, 2 * g)
        quantize_b(0, 0)
        quantize_b(0, 1)
        quantize_b(1, 0)
        quantize_b(1, 1)
        quantize_a(0, made[0])
        quantize_a(1, made[1])
        picked.append([gather_a(2, a, 8 + a) for a in range(PASSES)])
        made[2], made[3] = layer_a_wide(picked[1], 1, 4)
        scores(0, 0)
        scores(1, 2)
        quantize_a(2, made[2])
        quantize_a(3, made[3])
        picked.append([gather_a(3, a, 14 + a) for a in range(PASSES)])
        made[4], made[5] = layer_a_wide(picked[2], 2, 4)
        scores(2, 0)
        quantize_a(4, made[4])
        scores(3, 2, (0,))
        quantize_a(5, made[5])
        scores(3, 3, (1,))
        for g in range(GROUPS):
            layer_a(6, g, picked[3], made[6], 4 + g)
        scores(4, 6)
        quantize_a(6, made[6])
        scores(5, 0, (0,))
        layer_a(7, 0, picked[3], made[7], 3)
        layer_a(7, 1, picked[3], made[7], 6)
        quantize_group(7, 0, made[7])
        scores(5, 1, (1,))
        quantize_group(7, 1, made[7])
        scores(6, 2, (0,))
        scores(6, 4, (1,))
        scores(7, 5, (0,))
        scores(7, 1, (1,), 2)
